import numpy as np
import ml_dtypes


def mxq(x, axis, fmt="e4m3"):
    dtype, down = {"e4m3": (ml_dtypes.float8_e4m3fn, 7), "e5m2": (ml_dtypes.float8_e5m2, 14)}[fmt]
    v = np.moveaxis(np.asarray(x, np.float32).astype(ml_dtypes.bfloat16).astype(np.float64), axis, -1)
    blocks = v.reshape(v.shape[:-1] + (-1, 32))
    amax = np.abs(blocks).max(-1, keepdims=True)
    byte = np.maximum(np.where(amax > 0, np.frexp(amax)[1] - 1 + 127, 0) - down, 1)
    scale = np.exp2(byte - 127.0)
    codes = (blocks / scale).astype(np.float32).astype(dtype).astype(np.float64)
    return np.moveaxis((codes * scale).reshape(v.shape), -1, axis)


WIDE = False


def mx_kscale(k):
    if not WIDE:
        return np.ones(k)
    levels = np.array([30, -30])
    if k % 512:
        return np.exp2(np.random.permutation(np.resize(levels, k // 32))).repeat(32)
    a = np.empty((k // 512, 16))
    for p in range(k // 512):
        a[p, :8] = np.random.permutation(np.resize(levels, 8))
        for g in range(8):
            far = levels[np.abs(levels - a[p, g]) >= 10]
            a[p, g + 8] = far[np.random.randint(len(far))]
    return np.exp2(a.ravel()).repeat(32)


def f64(x):
    return np.asarray(x).astype(np.float64)


def striped(idx):
    return np.tile(idx.reshape(-1, 16).T, (8, 1)).astype(np.uint16)


def unstriped(offs):
    return offs[:16].T.reshape(-1).astype(np.int64)


def bf(x):
    return np.asarray(x, np.float32).astype(ml_dtypes.bfloat16)


E2M1 = np.array([0.0, 0.5, 1.0, 1.5, 2.0, 3.0, 4.0, 6.0, -0.0, -0.5, -1.0, -1.5, -2.0, -3.0, -4.0, -6.0])


def pack_weight(w, fmt):
    k, n = w.shape
    w = f64(bf(w)).reshape(k // 32, 32, n)
    amax = np.abs(w).max(1)
    if fmt in ("e4m3", "e5m2"):
        byte = np.frexp(amax)[1] - 1 + 127 - (7 if fmt == "e4m3" else 14)
    else:
        mant, ex = np.frexp(amax / 6.0)
        byte = np.where(mant > 0.5, ex, ex - 1) + 127
    byte = np.clip(np.where(amax > 0, byte, 1), 1, 254)
    scaled = (w * np.exp2(127.0 - byte)[:, None, :]).reshape(k, n).astype(np.float32)
    by_word = np.ascontiguousarray(scaled.reshape(k // 512, 128, 4, n).transpose(0, 1, 3, 2))
    if fmt in ("e4m3", "e5m2"):
        words = by_word.astype(ml_dtypes.float8_e4m3fn if fmt == "e4m3" else ml_dtypes.float8_e5m2).view(np.uint8)
    else:
        c = by_word.astype(ml_dtypes.float4_e2m1fn).view(np.uint8) & 0xF
        words = c[..., 0::2] | (c[..., 1::2] << 4)
    return np.ascontiguousarray(words), np.ascontiguousarray(byte.astype(np.uint8).reshape(k // 512, 16, n))


def unpack_weight(words, scales, fmt):
    g, p, n, _ = words.shape
    if fmt in ("e4m3", "e5m2"):
        vals = np.ascontiguousarray(words).view(ml_dtypes.float8_e4m3fn if fmt == "e4m3" else ml_dtypes.float8_e5m2).astype(np.float64)
    else:
        nib = np.empty((g, p, n, 4), np.uint8)
        nib[..., 0::2] = words & 0xF
        nib[..., 1::2] = words >> 4
        vals = E2M1[nib]
    vals = vals * np.repeat(np.exp2(scales.astype(np.float64) - 127.0), 8, axis=1)[..., None]
    return vals.transpose(0, 1, 3, 2).reshape(g * 512, n)


K, T, S, H, N = 1024, 2048, 1024, 1024, 512

def setup_inputs():
    n = np.random.standard_normal
    s = mx_kscale(K)[:, None]
    u = mx_kscale(H)[:, None]
    resid = n((K, T)) * np.exp(0.7 * n((1, T))) * s
    tab_words, tab_scales = pack_weight(resid, "e5m2")
    w3_words, w3_scales = pack_weight(n((H, N)) / np.sqrt(H) / u, "e4m3")
    return {
        "tab_words": tab_words,
        "tab_scales": tab_scales,
        "offs": striped(np.random.permutation(T)[:S]),
        "wr": (n((K, H)) / np.sqrt(K) / s * u.T).astype(np.float32),
        "wi": (n((K, H)) / np.sqrt(K) / s * u.T).astype(np.float32),
        "w3_words": w3_words,
        "w3_scales": w3_scales,
        "illum": np.exp(0.3 * n(N)).astype(np.float32),
    }

def reference(tab_words, tab_scales, offs, wr, wi, w3_words, w3_scales, illum):
    v = unpack_weight(tab_words, tab_scales, "e5m2")[:, unstriped(offs)]
    re = mxq(f64(wr), 0, "e4m3").T @ v
    im = mxq(f64(wi), 0, "e4m3").T @ v
    h = np.sqrt(re * re + im * im)
    hq = mxq(h, 0, "e4m3")
    w3 = unpack_weight(w3_words, w3_scales, "e4m3")
    y = w3.T @ hq
    return f64(illum)[:, None] * y

@@ -1,0 +1,276 @@
+from contextlib import ExitStack
+
+import concourse.mybir as mybir
+
+K, T, S, H, N = 1024, 2048, 1024, 1024, 512
+FLOPS = 2 * (2 * K * H * S + H * N * S)
+
+F32 = mybir.dt.float32
+BF16 = mybir.dt.bfloat16
+I32 = mybir.dt.int32
+U32 = mybir.dt.uint32
+U16 = mybir.dt.uint16
+U8 = mybir.dt.uint8
+E4M3 = mybir.dt.float8_e4m3fn_x4
+E5M2 = mybir.dt.float8_e5m2_x4
+ACT = mybir.ActivationFunctionType
+ALU = mybir.AluOpType
+
+P = 128
+PACK = 4
+PASS = P * PACK
+HALF = 512
+
+
+def tile_list_residual_envelope_map_kernel(
+    tc, tab_words, tab_scales, offs, wr, wi, w3_words, w3_scales, illum, out
+):
+    nc = tc.nc
+    with ExitStack() as ctx:
+        keep = ctx.enter_context(tc.tile_pool(name="keep", bufs=1))
+        stage = ctx.enter_context(tc.tile_pool(name="stage", bufs=2))
+        psum = ctx.enter_context(tc.psum_pool(name="psum", bufs=1))
+
+        offsets = keep.tile([P, S // 16], U16, name="offsets")
+        nc.sync.dma_start(offsets[:], offs)
+
+        scale_window = keep.tile([P, T], U8, name="scale_window", align_bytes=64)
+        nc.vector.memset(scale_window[:].bitcast(I32), 0)
+        weights = {"r": wr, "i": wi}
+        raw = {}
+
+        def load_weights(part, g, a):
+            held = stage.tile([P, PACK, PASS], F32, name="landing", align_bytes=64, bufs=4)
+            rows = weights[part][a * PASS : (a + 1) * PASS, g * PASS : (g + 1) * PASS]
+            nc.sync.dma_start(out=held[:], in_=rows.rearrange("(p j) c -> p j c", j=PACK))
+            raw[part, g, a] = held
+
+        table = []
+
+        def load_table(a):
+            held = stage.tile([P, T], U32, name="landing", align_bytes=64, bufs=4)
+            nc.sync.dma_start(
+                out=held[:].bitcast(I32), in_=tab_words[a].rearrange("p t i -> p (t i)").bitcast(I32)
+            )
+            table.append(held)
+
+        load_table(0)
+        by_row = tab_scales.rearrange("a (q r) t -> r q a t", r=4)
+        for r in range(4):
+            nc.sync.dma_start(out=scale_window[r:P:16, :].bitcast(I32), in_=by_row[r].bitcast(I32))
+        moved_scales = keep.tile([P, S], U8, name="moved_scales", align_bytes=64)
+        nc.vector.memset(moved_scales[:].bitcast(I32), 0)
+        w3_planes = keep.tile([P, N], U8, name="w3_planes", align_bytes=64)
+        nc.vector.memset(w3_planes[:].bitcast(I32), 0)
+        warm_in = keep.tile([P, 1], F32, name="warm_in")
+        warm_out = keep.tile([P, 1], F32, name="warm_out")
+        nc.vector.memset(warm_in[:], 1.0)
+        nc.scalar.activation(warm_out[:], warm_in[:], ACT.Sqrt)
+
+
+        load_weights("r", 0, 0)
+        load_table(1)
+        load_weights("r", 0, 1)
+        for q in range(4):
+            nc.gpsimd.dma_start(
+                out=w3_planes[32 * q : 32 * q + 8, :].bitcast(I32),
+                in_=w3_scales[:, 4 * q : 4 * q + 4, :].bitcast(I32),
+            )
+        gain = keep.tile([P, N // P], F32, name="gain")
+        with nc.allow_non_contiguous_dma(reason="one value of illum for each partition"):
+            nc.gpsimd.dma_start(out=gain[:], in_=illum.rearrange("(c p) -> p c", p=P))
+
+        picked_scales = keep.tile([P, S], U8, name="picked_scales", align_bytes=64)
+        nc.vector.tensor_copy(picked_scales[:], scale_window[:].indirect(offsets[:]))
+        nc.sync.dma_start(out=moved_scales[0:112, :].bitcast(I32), in_=picked_scales[16:P, :].bitcast(I32))
+        v_scales = [picked_scales, moved_scales]
+        load_weights("i", 0, 0)
+        load_weights("i", 0, 1)
+        load_weights("r", 1, 0)
+        load_weights("r", 1, 1)
+        load_weights("i", 1, 0)
+        load_weights("i", 1, 1)
+        w3_codes = stage.tile([P, 2, N], U32, name="landing", align_bytes=64, bufs=4)
+        nc.sync.dma_start(
+            out=w3_codes[:].bitcast(I32), in_=w3_words.rearrange("a p c i -> p a (c i)").bitcast(I32)
+        )
+
+        v_codes = {}
+
+        def gather_words(a, half):
+            held = keep.tile([P, HALF], U32, name="v_codes%d%d" % (a, half), align_bytes=64)
+            cols = slice(half * HALF // 16, (half + 1) * HALF // 16)
+            nc.vector.tensor_copy(held[:], table[a][:].indirect(offsets[:, cols]))
+            v_codes[a, half] = held
+
+        w_codes = {}
+        w_scales = {}
+
+        def quantize_weights(part, g, a, scalar_pairs):
+            key = (part, g, a)
+            w_codes[key] = keep.tile([P, PASS], U32, name="wc_%s%d%d" % key, align_bytes=64)
+            w_scales[key] = keep.tile([P, PASS], U8, name="ws_%s%d%d" % key, align_bytes=64)
+            source = raw[key][:].rearrange("p j (m t) -> p m j t", t=PACK)
+            rounded_pairs = []
+            for u in range(2):
+                pair = source[:, :, :, 2 * u : 2 * u + 2]
+                if u in scalar_pairs:
+                    grouped = stage.tile([P, 2, P, PACK], BF16, name="grouped_by_scalar", align_bytes=64, bufs=2)
+                    nc.scalar.copy(grouped[:].rearrange("p t m j -> p m j t"), pair)
+                else:
+                    grouped = stage.tile([P, 2, P, PACK], BF16, name="grouped", align_bytes=64, bufs=2)
+                    nc.vector.tensor_copy(grouped[:].rearrange("p t m j -> p m j t"), pair)
+                rounded_pairs.append(grouped)
+            for u in range(2):
+                cols = slice(2 * u * P, (2 * u + 2) * P)
+                nc.vector.quantize_mx(
+                    out=w_codes[key][:, cols].bitcast(E4M3),
+                    scales=w_scales[key][:, cols],
+                    in_=rounded_pairs[u][:].rearrange("p t m j -> p (t m j)"),
+                )
+
+        def filter_pass(acc, part, g, a, half, t):
+            cols = slice(t * P, (t + 1) * P)
+            nc.tensor.matmul_mx(
+                out=acc[:],
+                lhsT=w_codes[part, g, a][:, cols].bitcast(E4M3),
+                lhsT_scale=w_scales[part, g, a][:, cols],
+                rhs=v_codes[a, half][:].bitcast(E5M2),
+                rhs_scale=v_scales[a][:, half * HALF : (half + 1) * HALF],
+                start=(a == 0),
+                stop=(a == 1),
+            )
+
+        sums = {}
+        re_squared = {}
+        power = {}
+
+        def open_sums(part, g, slots):
+            for half, t in slots:
+                sums[part, g, half, t] = psum.tile([P, HALF], F32, name="acc", bufs=6)
+                filter_pass(sums[part, g, half, t], part, g, 0, half, t)
+
+        def close_sums(part, g, slots):
+            for half, t in slots:
+                acc = sums[part, g, half, t]
+                filter_pass(acc, part, g, 1, half, t)
+                if part == "r":
+                    re_squared[g, half, t] = stage.tile([P, HALF], F32, name="re_squared", bufs=12)
+                    nc.scalar.activation(re_squared[g, half, t][:], acc[:], ACT.Square)
+                else:
+                    if (g, half) not in power:
+                        power[g, half] = keep.tile([P, PACK, HALF], F32, name="power%d%d" % (g, half))
+                    nc.scalar.activation(power[g, half][:, t, :], acc[:], ACT.Square)
+
+        def whole_sums(part, g, slots):
+            for slot in slots:
+                open_sums(part, g, [slot])
+                close_sums(part, g, [slot])
+
+        def add_squares(g, half):
+            for t in range(PACK):
+                total = power[g, half][:, t, :]
+                nc.vector.tensor_tensor(total, total, re_squared[g, half, t][:], ALU.add)
+
+        h_codes = {}
+        h_scales = {}
+
+        rounded = {}
+
+        def square_root(g, half, first, width):
+            rounded[g, half, first] = stage.tile([P, width, PACK], BF16, name="rounded", align_bytes=64, bufs=3)
+            nc.scalar.activation(
+                rounded[g, half, first][:].rearrange("p (c i) t -> p c t i", i=4),
+                power[g, half][:, :, first : first + width].rearrange("p t (c i) -> p c t i", i=4),
+                ACT.Sqrt,
+            )
+
+        def quantize_envelope(g, half, first, width):
+            if first == 0:
+                h_codes[g, half] = keep.tile([P, HALF], U32, name="hc%d%d" % (g, half), align_bytes=64)
+                h_scales[g, half] = keep.tile([P, HALF], U8, name="hs%d%d" % (g, half), align_bytes=64)
+            cols = slice(first, first + width)
+            nc.vector.quantize_mx(
+                out=h_codes[g, half][:, cols].bitcast(E4M3),
+                scales=h_scales[g, half][:, cols],
+                in_=rounded[g, half, first][:].rearrange("p c t -> p (c t)"),
+            )
+
+        out_rows = out.rearrange("(c p) j -> p c j", p=P)
+
+        def model_cells(half, first, width, scalar_banks, bank_tag, banks):
+            cols = slice(first, first + width)
+            per_bank = HALF // width
+            for bank in range(N // P // per_bank):
+                acc = psum.tile([P, per_bank, width], F32, name=bank_tag, bufs=banks)
+                result = stage.tile([P, per_bank, width], F32, name="result", bufs=8)
+                for i in range(per_bank):
+                    c = bank * per_bank + i
+                    cells = slice(c * P, (c + 1) * P)
+                    for g in range(2):
+                        nc.tensor.matmul_mx(
+                            out=acc[:, i, :],
+                            lhsT=w3_codes[:, g, cells].bitcast(E4M3),
+                            lhsT_scale=w3_planes[4 * g : P, cells],
+                            rhs=h_codes[g, half][:, cols].bitcast(E4M3),
+                            rhs_scale=h_scales[g, half][:, cols],
+                            start=(g == 0),
+                            stop=(g == 1),
+                        )
+                for i in range(per_bank):
+                    c = bank * per_bank + i
+                    if bank in scalar_banks:
+                        nc.scalar.activation(result[:, i, :], acc[:, i, :], ACT.Copy, scale=gain[:, c : c + 1])
+                    else:
+                        nc.vector.tensor_scalar(result[:, i, :], acc[:, i, :], gain[:, c : c + 1], None, ALU.mult)
+                j0 = half * HALF + first
+                nc.sync.dma_start(
+                    out=out_rows[:, bank * per_bank : (bank + 1) * per_bank, j0 : j0 + width], in_=result[:]
+                )
+
+        halves = [[(half, t) for t in range(PACK)] for half in range(2)]
+        both = halves[0] + halves[1]
+        by_pairs = [(half, 2 * u + i) for u in range(2) for half in range(2) for i in range(2)]
+
+        gather_words(0, 0)
+        quantize_weights("r", 0, 0, (0, 1))
+        gather_words(0, 1)
+        open_sums("r", 0, by_pairs[:6])
+        gather_words(1, 0)
+        quantize_weights("r", 0, 1, (1,))
+        gather_words(1, 1)
+        close_sums("r", 0, by_pairs[:6])
+        whole_sums("r", 0, by_pairs[6:])
+
+        quantize_weights("i", 0, 0, ())
+        open_sums("i", 0, by_pairs[:6])
+        quantize_weights("i", 0, 1, ())
+        close_sums("i", 0, by_pairs[:6])
+        whole_sums("i", 0, by_pairs[6:])
+        add_squares(0, 0)
+        square_root(0, 0, 0, HALF)
+
+        quantize_weights("r", 1, 0, ())
+        quantize_weights("r", 1, 1, ())
+        open_sums("r", 1, halves[0])
+        close_sums("r", 1, halves[0])
+        quantize_weights("i", 1, 0, ())
+        quantize_weights("i", 1, 1, ())
+        quantize_envelope(0, 0, 0, HALF)
+        whole_sums("r", 1, halves[1])
+        for half in range(2):
+            whole_sums("i", 1, halves[half])
+            add_squares(1, half)
+        for first in (0, 256):
+            square_root(1, 0, first, 256)
+            quantize_envelope(1, 0, first, 256)
+        add_squares(0, 1)
+        square_root(0, 1, 0, HALF)
+        quantize_envelope(0, 1, 0, HALF)
+        for first in (0, 256):
+            square_root(1, 1, first, 256)
+            quantize_envelope(1, 1, first, 256)
+        for first in (0, 256):
+            model_cells(0, first, 256, (), "cells", 2)
+        for first in (0, 256):
+            model_cells(1, first, 256, (1,), "acc", 6)

@@ -20,6 +20,7 @@ P = 128
 PACK = 4
 PASS = P * PACK
 HALF = 512
+PIECE = 256
 
 
 def tile_list_residual_envelope_map_kernel(
@@ -34,7 +35,7 @@ def tile_list_residual_envelope_map_kernel(
         offsets = keep.tile([P, S // 16], U16, name="offsets")
         nc.sync.dma_start(offsets[:], offs)
 
-        scale_window = keep.tile([P, T], U8, name="scale_window", align_bytes=64)
+        scale_window = stage.tile([P, T], U8, name="landing", align_bytes=64, bufs=4)
         nc.vector.memset(scale_window[:].bitcast(I32), 0)
         weights = {"r": wr, "i": wi}
         raw = {}
@@ -48,7 +49,10 @@ def tile_list_residual_envelope_map_kernel(
         table = []
 
         def load_table(a):
-            held = stage.tile([P, T], U32, name="landing", align_bytes=64, bufs=4)
+            if a == 0:
+                held = keep.tile([P, T], U32, name="first_table", align_bytes=64)
+            else:
+                held = stage.tile([P, T], U32, name="landing", align_bytes=64, bufs=4)
             nc.sync.dma_start(
                 out=held[:].bitcast(I32), in_=tab_words[a].rearrange("p t i -> p (t i)").bitcast(I32)
             )
@@ -129,7 +133,7 @@ def tile_list_residual_envelope_map_kernel(
                     in_=rounded_pairs[u][:].rearrange("p t m j -> p (t m j)"),
                 )
 
-        def filter_pass(acc, part, g, a, half, t):
+        def filter_pass(acc, part, g, a, half, t, opens):
             cols = slice(t * P, (t + 1) * P)
             nc.tensor.matmul_mx(
                 out=acc[:],
@@ -137,40 +141,49 @@ def tile_list_residual_envelope_map_kernel(
                 lhsT_scale=w_scales[part, g, a][:, cols],
                 rhs=v_codes[a, half][:].bitcast(E5M2),
                 rhs_scale=v_scales[a][:, half * HALF : (half + 1) * HALF],
-                start=(a == 0),
-                stop=(a == 1),
+                start=opens,
+                stop=not opens,
             )
 
         sums = {}
-        re_squared = {}
+        squares = {}
         power = {}
 
-        def open_sums(part, g, slots):
+        def open_sums(part, g, slots, a):
             for half, t in slots:
                 sums[part, g, half, t] = psum.tile([P, HALF], F32, name="acc", bufs=6)
-                filter_pass(sums[part, g, half, t], part, g, 0, half, t)
+                filter_pass(sums[part, g, half, t], part, g, a, half, t, True)
 
-        def close_sums(part, g, slots):
+        def close_sums(part, g, slots, a):
             for half, t in slots:
                 acc = sums[part, g, half, t]
-                filter_pass(acc, part, g, 1, half, t)
-                if part == "r":
-                    re_squared[g, half, t] = stage.tile([P, HALF], F32, name="re_squared", bufs=12)
-                    nc.scalar.activation(re_squared[g, half, t][:], acc[:], ACT.Square)
-                else:
-                    if (g, half) not in power:
-                        power[g, half] = keep.tile([P, PACK, HALF], F32, name="power%d%d" % (g, half))
-                    nc.scalar.activation(power[g, half][:, t, :], acc[:], ACT.Square)
+                filter_pass(acc, part, g, a, half, t, False)
+                key = (part, g, half, t // 2)
+                if key not in squares:
+                    squares[key] = stage.tile([P, 2, HALF], F32, name="squares", bufs=12)
+                nc.scalar.activation(squares[key][:, t % 2, :], acc[:], ACT.Square)
 
-        def whole_sums(part, g, slots):
+        def filter_stage(part, g, slots, early):
+            open_sums(part, g, slots[:early], 0)
+            if (part, g, 1) not in w_codes:
+                quantize_weights(part, g, 1, ())
+            close_sums(part, g, slots[:early], 1)
+            late_sums(part, g, slots[early:])
+
+        def late_sums(part, g, slots):
             for slot in slots:
-                open_sums(part, g, [slot])
-                close_sums(part, g, [slot])
+                open_sums(part, g, [slot], 1)
+                close_sums(part, g, [slot], 0)
 
         def add_squares(g, half):
-            for t in range(PACK):
-                total = power[g, half][:, t, :]
-                nc.vector.tensor_tensor(total, total, re_squared[g, half, t][:], ALU.add)
+            power[g, half] = keep.tile([P, HALF // 2, 2, 2, 2], F32, name="power%d%d" % (g, half))
+            for u in range(2):
+                nc.vector.tensor_tensor(
+                    power[g, half][:, :, u, :, :],
+                    squares["r", g, half, u][:].rearrange("p t (c i) -> p c t i", i=2),
+                    squares["i", g, half, u][:].rearrange("p t (c i) -> p c t i", i=2),
+                    ALU.add,
+                )
 
         h_codes = {}
         h_scales = {}
@@ -178,10 +191,10 @@ def tile_list_residual_envelope_map_kernel(
         rounded = {}
 
         def square_root(g, half, first, width):
-            rounded[g, half, first] = stage.tile([P, width, PACK], BF16, name="rounded", align_bytes=64, bufs=3)
+            rounded[g, half, first] = stage.tile([P, width, PACK], BF16, name="rounded", align_bytes=64, bufs=5)
             nc.scalar.activation(
-                rounded[g, half, first][:].rearrange("p (c i) t -> p c t i", i=4),
-                power[g, half][:, :, first : first + width].rearrange("p t (c i) -> p c t i", i=4),
+                rounded[g, half, first][:].rearrange("p (c i) t -> p c i t", i=2),
+                power[g, half][:, first // 2 : (first + width) // 2].rearrange("p c u t i -> p c i (u t)"),
                 ACT.Sqrt,
             )
 
@@ -198,35 +211,53 @@ def tile_list_residual_envelope_map_kernel(
 
         out_rows = out.rearrange("(c p) j -> p c j", p=P)
 
-        def model_cells(half, first, width, scalar_banks, bank_tag, banks):
-            cols = slice(first, first + width)
-            per_bank = HALF // width
-            for bank in range(N // P // per_bank):
-                acc = psum.tile([P, per_bank, width], F32, name=bank_tag, bufs=banks)
-                result = stage.tile([P, per_bank, width], F32, name="result", bufs=8)
-                for i in range(per_bank):
-                    c = bank * per_bank + i
-                    cells = slice(c * P, (c + 1) * P)
+        def cell_pass(acc, c, g, half, cols):
+            cells = slice(c * P, (c + 1) * P)
+            nc.tensor.matmul_mx(
+                out=acc,
+                lhsT=w3_codes[:, g, cells].bitcast(E4M3),
+                lhsT_scale=w3_planes[4 * g : P, cells],
+                rhs=h_codes[g, half][:, cols].bitcast(E4M3),
+                rhs_scale=h_scales[g, half][:, cols],
+                start=(g == 0),
+                stop=(g == 1),
+            )
+
+        def store_pair(result, pair, half, first):
+            j0 = half * HALF + first
+            nc.sync.dma_start(out=out_rows[:, 2 * pair : 2 * pair + 2, j0 : j0 + PIECE], in_=result[:])
+
+        def cells_two_to_a_bank(half, first):
+            cols = slice(first, first + PIECE)
+            for pair in range(2):
+                acc = psum.tile([P, 2, PIECE], F32, name="cells", bufs=2)
+                for i in range(2):
                     for g in range(2):
-                        nc.tensor.matmul_mx(
-                            out=acc[:, i, :],
-                            lhsT=w3_codes[:, g, cells].bitcast(E4M3),
-                            lhsT_scale=w3_planes[4 * g : P, cells],
-                            rhs=h_codes[g, half][:, cols].bitcast(E4M3),
-                            rhs_scale=h_scales[g, half][:, cols],
-                            start=(g == 0),
-                            stop=(g == 1),
-                        )
-                for i in range(per_bank):
-                    c = bank * per_bank + i
-                    if bank in scalar_banks:
-                        nc.scalar.activation(result[:, i, :], acc[:, i, :], ACT.Copy, scale=gain[:, c : c + 1])
+                        cell_pass(acc[:, i, :], 2 * pair + i, g, half, cols)
+                result = stage.tile([P, 2, PIECE], F32, name="result", bufs=8)
+                spread = gain[:, 2 * pair : 2 * pair + 2].unsqueeze(2).to_broadcast([P, 2, PIECE])
+                nc.vector.tensor_tensor(result[:], acc[:], spread, ALU.mult)
+                store_pair(result, pair, half, first)
+
+        def cells_one_to_a_bank(half, first, shared):
+            cols = slice(first, first + PIECE)
+            accs = [psum.tile([P, PIECE], F32, name="acc", bufs=6) for c in range(4)]
+            for c in range(4):
+                cell_pass(accs[c][:], c, 0, half, cols)
+            for pair in range(2):
+                result = stage.tile([P, 2, PIECE], F32, name="result", bufs=8)
+                for i in range(2):
+                    c = 2 * pair + i
+                    cell_pass(accs[c][:], c, 1, half, cols)
+                    if shared and i == 1:
+                        nc.scalar.activation(result[:, i, :], accs[c][:], ACT.Copy, scale=gain[:, c : c + 1])
                     else:
-                        nc.vector.tensor_scalar(result[:, i, :], acc[:, i, :], gain[:, c : c + 1], None, ALU.mult)
-                j0 = half * HALF + first
-                nc.sync.dma_start(
-                    out=out_rows[:, bank * per_bank : (bank + 1) * per_bank, j0 : j0 + width], in_=result[:]
-                )
+                        nc.vector.tensor_scalar(result[:, i, :], accs[c][:], gain[:, c : c + 1], None, ALU.mult)
+                store_pair(result, pair, half, first)
+
+        def envelope(g, half, first):
+            square_root(g, half, first, PIECE)
+            quantize_envelope(g, half, first, PIECE)
 
         halves = [[(half, t) for t in range(PACK)] for half in range(2)]
         both = halves[0] + halves[1]
@@ -235,42 +266,35 @@ def tile_list_residual_envelope_map_kernel(
         gather_words(0, 0)
         quantize_weights("r", 0, 0, (0, 1))
         gather_words(0, 1)
-        open_sums("r", 0, by_pairs[:6])
+        open_sums("r", 0, by_pairs[:4], 0)
         gather_words(1, 0)
         quantize_weights("r", 0, 1, (1,))
         gather_words(1, 1)
-        close_sums("r", 0, by_pairs[:6])
-        whole_sums("r", 0, by_pairs[6:])
+        close_sums("r", 0, by_pairs[:4], 1)
+        late_sums("r", 0, by_pairs[4:])
 
         quantize_weights("i", 0, 0, ())
-        open_sums("i", 0, by_pairs[:6])
-        quantize_weights("i", 0, 1, ())
-        close_sums("i", 0, by_pairs[:6])
-        whole_sums("i", 0, by_pairs[6:])
+        filter_stage("i", 0, both, 2)
         add_squares(0, 0)
         square_root(0, 0, 0, HALF)
 
         quantize_weights("r", 1, 0, ())
-        quantize_weights("r", 1, 1, ())
-        open_sums("r", 1, halves[0])
-        close_sums("r", 1, halves[0])
+        filter_stage("r", 1, halves[0], 2)
         quantize_weights("i", 1, 0, ())
         quantize_weights("i", 1, 1, ())
         quantize_envelope(0, 0, 0, HALF)
-        whole_sums("r", 1, halves[1])
-        for half in range(2):
-            whole_sums("i", 1, halves[half])
-            add_squares(1, half)
-        for first in (0, 256):
-            square_root(1, 0, first, 256)
-            quantize_envelope(1, 0, first, 256)
         add_squares(0, 1)
-        square_root(0, 1, 0, HALF)
-        quantize_envelope(0, 1, 0, HALF)
-        for first in (0, 256):
-            square_root(1, 1, first, 256)
-            quantize_envelope(1, 1, first, 256)
-        for first in (0, 256):
-            model_cells(0, first, 256, (), "cells", 2)
-        for first in (0, 256):
-            model_cells(1, first, 256, (1,), "acc", 6)
+        late_sums("r", 1, halves[1])
+        late_sums("i", 1, halves[0])
+        add_squares(1, 0)
+        envelope(1, 0, 0)
+        late_sums("i", 1, halves[1])
+        add_squares(1, 1)
+        envelope(1, 0, PIECE)
+        for first in (0, PIECE):
+            cells_two_to_a_bank(0, first)
+        for first in (0, PIECE):
+            envelope(0, 1, first)
+            envelope(1, 1, first)
+        for first in (0, PIECE):
+            cells_one_to_a_bank(1, first, first > 0)

@@ -53,9 +53,10 @@ def tile_list_residual_envelope_map_kernel(
                 held = keep.tile([P, T], U32, name="first_table", align_bytes=64)
             else:
                 held = stage.tile([P, T], U32, name="landing", align_bytes=64, bufs=4)
-            nc.sync.dma_start(
-                out=held[:].bitcast(I32), in_=tab_words[a].rearrange("p t i -> p (t i)").bitcast(I32)
-            )
+            words = tab_words[a].rearrange("p t i -> p (t i)").bitcast(I32)
+            width = T // 2 if a == 0 else T
+            for c0 in range(0, T, width):
+                nc.sync.dma_start(out=held[:].bitcast(I32)[:, c0 : c0 + width], in_=words[:, c0 : c0 + width])
             table.append(held)
 
         load_table(0)
@@ -64,8 +65,6 @@ def tile_list_residual_envelope_map_kernel(
             nc.sync.dma_start(out=scale_window[r:P:16, :].bitcast(I32), in_=by_row[r].bitcast(I32))
         moved_scales = keep.tile([P, S], U8, name="moved_scales", align_bytes=64)
         nc.vector.memset(moved_scales[:].bitcast(I32), 0)
-        w3_planes = keep.tile([P, N], U8, name="w3_planes", align_bytes=64)
-        nc.vector.memset(w3_planes[:].bitcast(I32), 0)
         warm_in = keep.tile([P, 1], F32, name="warm_in")
         warm_out = keep.tile([P, 1], F32, name="warm_out")
         nc.vector.memset(warm_in[:], 1.0)
@@ -75,14 +74,6 @@ def tile_list_residual_envelope_map_kernel(
         load_weights("r", 0, 0)
         load_table(1)
         load_weights("r", 0, 1)
-        for q in range(4):
-            nc.gpsimd.dma_start(
-                out=w3_planes[32 * q : 32 * q + 8, :].bitcast(I32),
-                in_=w3_scales[:, 4 * q : 4 * q + 4, :].bitcast(I32),
-            )
-        gain = keep.tile([P, N // P], F32, name="gain")
-        with nc.allow_non_contiguous_dma(reason="one value of illum for each partition"):
-            nc.gpsimd.dma_start(out=gain[:], in_=illum.rearrange("(c p) -> p c", p=P))
 
         picked_scales = keep.tile([P, S], U8, name="picked_scales", align_bytes=64)
         nc.vector.tensor_copy(picked_scales[:], scale_window[:].indirect(offsets[:]))
@@ -98,6 +89,16 @@ def tile_list_residual_envelope_map_kernel(
         nc.sync.dma_start(
             out=w3_codes[:].bitcast(I32), in_=w3_words.rearrange("a p c i -> p a (c i)").bitcast(I32)
         )
+        w3_planes = stage.tile([P, N], U8, name="landing", align_bytes=64, bufs=4)
+        nc.vector.memset(w3_planes[:].bitcast(I32), 0)
+        for q in range(4):
+            nc.sync.dma_start(
+                out=w3_planes[32 * q : 32 * q + 8, :].bitcast(I32),
+                in_=w3_scales[:, 4 * q : 4 * q + 4, :].bitcast(I32),
+            )
+        gain = stage.tile([P, N // P], F32, name="landing", align_bytes=64, bufs=4)
+        with nc.allow_non_contiguous_dma(reason="one value of illum for each partition"):
+            nc.sync.dma_start(out=gain[:], in_=illum.rearrange("(c p) -> p c", p=P))
 
         v_codes = {}
 

@@ -1,6 +1,7 @@
 from contextlib import ExitStack
 
 import concourse.mybir as mybir
+from concourse.masks import make_identity
 
 K, T, S, H, N = 1024, 2048, 1024, 1024, 512
 FLOPS = 2 * (2 * K * H * S + H * N * S)
@@ -19,8 +20,11 @@ ALU = mybir.AluOpType
 P = 128
 PACK = 4
 PASS = P * PACK
-HALF = 512
-PIECE = 256
+QUARTER = 256
+QUARTERS = S // QUARTER
+STRIP = 256
+BANKS = 4
+TENSOR_QUARTERS = 2
 
 
 def tile_list_residual_envelope_map_kernel(
@@ -35,31 +39,8 @@ def tile_list_residual_envelope_map_kernel(
         offsets = keep.tile([P, S // 16], U16, name="offsets")
         nc.sync.dma_start(offsets[:], offs)
 
-        scale_window = stage.tile([P, T], U8, name="landing", align_bytes=64, bufs=4)
+        scale_window = keep.tile([P, T], U8, name="late_loads", align_bytes=64)
         nc.vector.memset(scale_window[:].bitcast(I32), 0)
-        weights = {"r": wr, "i": wi}
-        raw = {}
-
-        def load_weights(part, g, a):
-            held = stage.tile([P, PACK, PASS], F32, name="landing", align_bytes=64, bufs=4)
-            rows = weights[part][a * PASS : (a + 1) * PASS, g * PASS : (g + 1) * PASS]
-            nc.sync.dma_start(out=held[:], in_=rows.rearrange("(p j) c -> p j c", j=PACK))
-            raw[part, g, a] = held
-
-        table = []
-
-        def load_table(a):
-            if a == 0:
-                held = keep.tile([P, T], U32, name="first_table", align_bytes=64)
-            else:
-                held = stage.tile([P, T], U32, name="landing", align_bytes=64, bufs=4)
-            words = tab_words[a].rearrange("p t i -> p (t i)").bitcast(I32)
-            width = T // 2 if a == 0 else T
-            for c0 in range(0, T, width):
-                nc.sync.dma_start(out=held[:].bitcast(I32)[:, c0 : c0 + width], in_=words[:, c0 : c0 + width])
-            table.append(held)
-
-        load_table(0)
         by_row = tab_scales.rearrange("a (q r) t -> r q a t", r=4)
         for r in range(4):
             nc.sync.dma_start(out=scale_window[r:P:16, :].bitcast(I32), in_=by_row[r].bitcast(I32))
@@ -69,233 +50,348 @@ def tile_list_residual_envelope_map_kernel(
         warm_out = keep.tile([P, 1], F32, name="warm_out")
         nc.vector.memset(warm_in[:], 1.0)
         nc.scalar.activation(warm_out[:], warm_in[:], ACT.Sqrt)
+        identity = keep.tile([P, P], F32, name="identity")
+        make_identity(nc, identity[:])
 
+        weights = {"r": wr, "i": wi}
+        raw = {}
+        table = []
 
-        load_weights("r", 0, 0)
-        load_table(1)
-        load_weights("r", 0, 1)
+        def load_table(a, cuts):
+            held = keep.tile([P, T], U32, name="table%d" % a, align_bytes=64)
+            words = tab_words[a].rearrange("p t i -> p (t i)").bitcast(I32)
+            for c0, c1 in zip(cuts[:-1], cuts[1:]):
+                nc.sync.dma_start(out=held[:].bitcast(I32)[:, c0:c1], in_=words[:, c0:c1])
+            table.append(held)
+
+        def load_weights(held, part, c0, width, a):
+            rows = weights[part][a * PASS : (a + 1) * PASS, c0 : c0 + width]
+            view = held.rearrange("p (j c) -> p j c", j=PACK)
+            nc.sync.dma_start(out=view, in_=rows.rearrange("(p j) c -> p j c", j=PACK))
+            raw[part, c0, a] = view
+
+        load_table(0, (0, 256, 512, T))
+        for a in range(2):
+            if a == 1:
+                load_table(1, (0, T))
+            first = keep.tile([P, PACK * STRIP], F32, name="first_strip%d" % a, align_bytes=64)
+            load_weights(first[:], "r", 0, STRIP, a)
 
         picked_scales = keep.tile([P, S], U8, name="picked_scales", align_bytes=64)
         nc.vector.tensor_copy(picked_scales[:], scale_window[:].indirect(offsets[:]))
         nc.sync.dma_start(out=moved_scales[0:112, :].bitcast(I32), in_=picked_scales[16:P, :].bitcast(I32))
         v_scales = [picked_scales, moved_scales]
-        load_weights("i", 0, 0)
-        load_weights("i", 0, 1)
-        load_weights("r", 1, 0)
-        load_weights("r", 1, 1)
-        load_weights("i", 1, 0)
-        load_weights("i", 1, 1)
-        w3_codes = stage.tile([P, 2, N], U32, name="landing", align_bytes=64, bufs=4)
-        nc.sync.dma_start(
-            out=w3_codes[:].bitcast(I32), in_=w3_words.rearrange("a p c i -> p a (c i)").bitcast(I32)
-        )
-        w3_planes = stage.tile([P, N], U8, name="landing", align_bytes=64, bufs=4)
-        nc.vector.memset(w3_planes[:].bitcast(I32), 0)
-        for q in range(4):
-            nc.sync.dma_start(
-                out=w3_planes[32 * q : 32 * q + 8, :].bitcast(I32),
-                in_=w3_scales[:, 4 * q : 4 * q + 4, :].bitcast(I32),
-            )
-        gain = stage.tile([P, N // P], F32, name="landing", align_bytes=64, bufs=4)
-        with nc.allow_non_contiguous_dma(reason="one value of illum for each partition"):
-            nc.sync.dma_start(out=gain[:], in_=illum.rearrange("(c p) -> p c", p=P))
 
-        v_codes = {}
+        late = [("i", 0, STRIP), ("r", STRIP, STRIP), ("i", STRIP, STRIP), ("r", PASS, PASS), ("i", PASS, PASS)]
+        landing = keep.tile([P, sum(2 * PACK * w for part, c0, w in late)], F32, name="late_loads", align_bytes=64)
+        at = 0
+        for part, c0, width in late:
+            for a in range(2):
+                load_weights(landing[:, at : at + PACK * width], part, c0, width, a)
+                at = at + PACK * width
 
-        def gather_words(a, half):
-            held = keep.tile([P, HALF], U32, name="v_codes%d%d" % (a, half), align_bytes=64)
-            cols = slice(half * HALF // 16, (half + 1) * HALF // 16)
-            nc.vector.tensor_copy(held[:], table[a][:].indirect(offsets[:, cols]))
-            v_codes[a, half] = held
+        v_codes = [keep.tile([P, S], U32, name="v_codes%d" % a, align_bytes=64) for a in range(2)]
+
+        def gather_words(a, j0, count):
+            picks = offsets[:, j0 // 16 : (j0 + count) // 16]
+            nc.vector.tensor_copy(v_codes[a][:, j0 : j0 + count], table[a][:].indirect(picks))
 
         w_codes = {}
         w_scales = {}
+        grouped = {}
 
-        def quantize_weights(part, g, a, scalar_pairs):
-            key = (part, g, a)
-            w_codes[key] = keep.tile([P, PASS], U32, name="wc_%s%d%d" % key, align_bytes=64)
-            w_scales[key] = keep.tile([P, PASS], U8, name="ws_%s%d%d" % key, align_bytes=64)
-            source = raw[key][:].rearrange("p j (m t) -> p m j t", t=PACK)
-            rounded_pairs = []
+        def round_strip(part, c0, a, on_scalar):
             for u in range(2):
-                pair = source[:, :, :, 2 * u : 2 * u + 2]
-                if u in scalar_pairs:
-                    grouped = stage.tile([P, 2, P, PACK], BF16, name="grouped_by_scalar", align_bytes=64, bufs=2)
-                    nc.scalar.copy(grouped[:].rearrange("p t m j -> p m j t"), pair)
+                key = (part, c0, a, u)
+                if key == ("i", STRIP, 1, 1):
+                    grouped[key] = keep.tile([P, P * PACK], BF16, name="after_strips", align_bytes=64)
                 else:
-                    grouped = stage.tile([P, 2, P, PACK], BF16, name="grouped", align_bytes=64, bufs=2)
-                    nc.vector.tensor_copy(grouped[:].rearrange("p t m j -> p m j t"), pair)
-                rounded_pairs.append(grouped)
+                    name = "strip_by_scalar" if on_scalar else "strip_by_vector"
+                    grouped[key] = stage.tile([P, P * PACK], BF16, name=name, align_bytes=64, bufs=4)
+                target = grouped[key][:].rearrange("p (c i j) -> p c j i", i=4, j=PACK)
+                source = raw[part, c0, a][:, :, u * P : (u + 1) * P].rearrange("p j (c i) -> p c j i", i=4)
+                if on_scalar:
+                    nc.scalar.copy(target, source)
+                else:
+                    nc.vector.tensor_copy(target, source)
+
+        def quantize_strip(part, c0, a):
+            key = (part, c0, a)
+            w_codes[key] = keep.tile([P, STRIP], U32, name="wc_%s%d_%d" % key, align_bytes=64)
+            w_scales[key] = keep.tile([P, STRIP], U8, name="ws_%s%d_%d" % key, align_bytes=64)
+            for u in range(2):
+                cols = slice(u * P, (u + 1) * P)
+                nc.vector.quantize_mx(
+                    out=w_codes[key][:, cols].bitcast(E4M3),
+                    scales=w_scales[key][:, cols],
+                    in_=grouped[part, c0, a, u][:],
+                )
+
+        def prepare_strip(part, c0):
+            for a in range(2):
+                round_strip(part, c0, a, False)
+                quantize_strip(part, c0, a)
+
+        def strip_pass(acc, part, c0, a, q, i, start, stop):
+            cols = slice(q * QUARTER + i * P, q * QUARTER + (i + 1) * P)
+            nc.tensor.matmul_mx(
+                out=acc[:, i, :],
+                lhsT=v_codes[a][:, cols].bitcast(E5M2),
+                lhsT_scale=v_scales[a][:, cols],
+                rhs=w_codes[part, c0, a][:].bitcast(E4M3),
+                rhs_scale=w_scales[part, c0, a][:],
+                start=start,
+                stop=stop,
+            )
+
+        turned_squares = {}
+
+        def square_strip(acc, part, c0, q):
+            if (part, q) not in turned_squares:
+                turned_squares[part, q] = keep.tile([P, 2, PACK, P], F32, name="turned_%s%d" % (part, q))
+            m0 = c0 // PACK
+            nc.scalar.activation(
+                turned_squares[part, q][:, :, :, m0 : m0 + STRIP // PACK],
+                acc[:].rearrange("p i (m t) -> p i t m", t=PACK),
+                ACT.Square,
+            )
+
+        def strip_sums(part, c0, q):
+            acc = psum.tile([P, 2, STRIP], F32, name="sums", bufs=BANKS)
+            for i in range(2):
+                for a in (1, 0):
+                    strip_pass(acc, part, c0, a, q, i, a == 1, a == 0)
+            square_strip(acc, part, c0, q)
+
+        vector_sums = {}
+
+        def add_strip(q, c0, width, follows):
+            if c0 == 0:
+                vector_sums[q] = keep.tile([P, 2, PACK, P], F32, name=follows, align_bytes=64)
+            ms = slice(c0 // PACK, (c0 + width) // PACK)
+            nc.vector.tensor_tensor(
+                vector_sums[q][:, :, :, ms],
+                turned_squares["r", q][:, :, :, ms],
+                turned_squares["i", q][:, :, :, ms],
+                ALU.add,
+            )
+
+        rounded = {}
+        h_codes = [keep.tile([P, S], U32, name="h_codes%d" % g, align_bytes=64) for g in range(2)]
+        h_scales = [keep.tile([P, S], U8, name="h_scales1", align_bytes=64)]
+
+        def turn_and_root(q, tiles=(0, 1)):
+            if 0 in tiles:
+                rounded[0, q * QUARTER] = stage.tile([P, QUARTER, PACK], BF16, name="rounded0", align_bytes=64, bufs=2)
+            if q < TENSOR_QUARTERS:
+                terms = [turned_squares["i", q][:], turned_squares["r", q][:]]
+            else:
+                terms = [vector_sums[q][:]]
+            for i in tiles:
+                turned = psum.tile([P, PACK, P], F32, name="turns", bufs=BANKS)
+                for t in range(PACK):
+                    for n, term in enumerate(terms):
+                        nc.tensor.matmul(
+                            turned[:, t, :],
+                            term[:, i, t, :],
+                            identity[:],
+                            start=(n == 0),
+                            stop=(n == len(terms) - 1),
+                            is_transpose=True,
+                        )
+                nc.scalar.activation(
+                    rounded[0, q * QUARTER][:, i * P : (i + 1) * P, :],
+                    turned[:].rearrange("p t j -> p j t"),
+                    ACT.Sqrt,
+                )
+
+        def quantize_envelope(g, j0, width):
+            cols = slice(j0, j0 + width)
+            nc.vector.quantize_mx(
+                out=h_codes[g][:, cols].bitcast(E4M3),
+                scales=h_scales[g][:, cols],
+                in_=rounded[g, j0][:].rearrange("p c t -> p (c t)"),
+            )
+
+        def quantize_block(part, a):
+            key = (part, PASS, a)
+            w_codes[key] = keep.tile([P, PASS], U32, name="wc_%s%d_%d" % key, align_bytes=64)
+            w_scales[key] = keep.tile([P, PASS], U8, name="ws_%s%d_%d" % key, align_bytes=64)
+            source = raw[key].rearrange("p j (m t) -> p m j t", t=PACK)
+            pairs = []
+            for u in range(2):
+                if (part, a) == ("i", 1):
+                    pair = keep.tile([P, 2, P, PACK], BF16, name="after_block%d" % u, align_bytes=64)
+                else:
+                    pair = stage.tile([P, 2, P, PACK], BF16, name="block_pair", align_bytes=64, bufs=2)
+                nc.vector.tensor_copy(pair[:].rearrange("p t m j -> p m j t"), source[:, :, :, 2 * u : 2 * u + 2])
+                pairs.append(pair)
             for u in range(2):
                 cols = slice(2 * u * P, (2 * u + 2) * P)
                 nc.vector.quantize_mx(
                     out=w_codes[key][:, cols].bitcast(E4M3),
                     scales=w_scales[key][:, cols],
-                    in_=rounded_pairs[u][:].rearrange("p t m j -> p (t m j)"),
+                    in_=pairs[u][:].rearrange("p t m j -> p (t m j)"),
                 )
 
-        def filter_pass(acc, part, g, a, half, t, opens):
-            cols = slice(t * P, (t + 1) * P)
+        squares = {}
+
+        def block_pass(acc, part, a, t, cols, start, stop):
+            rows = slice(t * P, (t + 1) * P)
             nc.tensor.matmul_mx(
-                out=acc[:],
-                lhsT=w_codes[part, g, a][:, cols].bitcast(E4M3),
-                lhsT_scale=w_scales[part, g, a][:, cols],
-                rhs=v_codes[a, half][:].bitcast(E5M2),
-                rhs_scale=v_scales[a][:, half * HALF : (half + 1) * HALF],
-                start=opens,
-                stop=not opens,
+                out=acc,
+                lhsT=w_codes[part, PASS, a][:, rows].bitcast(E4M3),
+                lhsT_scale=w_scales[part, PASS, a][:, rows],
+                rhs=v_codes[a][:, cols].bitcast(E5M2),
+                rhs_scale=v_scales[a][:, cols],
+                start=start,
+                stop=stop,
             )
 
-        sums = {}
-        squares = {}
+        def open_bank(part, j0, width, t0, a):
+            per_bank = PASS // width
+            acc = psum.tile([P, per_bank, width], F32, name="sums", bufs=BANKS)
+            for i in range(per_bank):
+                block_pass(acc[:, i, :], part, a, t0 + i, slice(j0, j0 + width), i == 0, False)
+            return acc
+
+        def close_bank(acc, part, j0, width, t0, a):
+            per_bank = PASS // width
+            if t0 == 0:
+                squares[part, j0] = stage.tile([P, PACK, width], F32, name="squares_" + part, bufs=3 if part == "r" else 2)
+            for i in range(per_bank):
+                block_pass(acc[:, i, :], part, a, t0 + i, slice(j0, j0 + width), False, i == per_bank - 1)
+            nc.scalar.activation(squares[part, j0][:, t0 : t0 + per_bank, :], acc[:], ACT.Square)
+
+        def block_sums(part, j0, width):
+            first = 0 if j0 == 0 else 1
+            for t0 in range(0, PACK, PASS // width):
+                close_bank(open_bank(part, j0, width, t0, first), part, j0, width, t0, 1 - first)
+
         power = {}
 
-        def open_sums(part, g, slots, a):
-            for half, t in slots:
-                sums[part, g, half, t] = psum.tile([P, HALF], F32, name="acc", bufs=6)
-                filter_pass(sums[part, g, half, t], part, g, a, half, t, True)
-
-        def close_sums(part, g, slots, a):
-            for half, t in slots:
-                acc = sums[part, g, half, t]
-                filter_pass(acc, part, g, a, half, t, False)
-                key = (part, g, half, t // 2)
-                if key not in squares:
-                    squares[key] = stage.tile([P, 2, HALF], F32, name="squares", bufs=12)
-                nc.scalar.activation(squares[key][:, t % 2, :], acc[:], ACT.Square)
-
-        def filter_stage(part, g, slots, early):
-            open_sums(part, g, slots[:early], 0)
-            if (part, g, 1) not in w_codes:
-                quantize_weights(part, g, 1, ())
-            close_sums(part, g, slots[:early], 1)
-            late_sums(part, g, slots[early:])
-
-        def late_sums(part, g, slots):
-            for slot in slots:
-                open_sums(part, g, [slot], 1)
-                close_sums(part, g, [slot], 0)
-
-        def add_squares(g, half):
-            power[g, half] = keep.tile([P, HALF // 2, 2, 2, 2], F32, name="power%d%d" % (g, half))
-            for u in range(2):
+        def add_block(j0, width):
+            power[j0] = stage.tile([P, width // 2, PACK, 2], F32, name="power", bufs=2)
+            per_bank = PASS // width
+            q0 = j0 // QUARTER * QUARTER
+            for t0 in range(0, PACK, per_bank):
+                ts = slice(t0, t0 + per_bank)
                 nc.vector.tensor_tensor(
-                    power[g, half][:, :, u, :, :],
-                    squares["r", g, half, u][:].rearrange("p t (c i) -> p c t i", i=2),
-                    squares["i", g, half, u][:].rearrange("p t (c i) -> p c t i", i=2),
+                    power[j0][:, :, ts, :],
+                    squares["r", q0][:, ts, j0 - q0 : j0 - q0 + width].rearrange("p t (c i) -> p c t i", i=2),
+                    squares["i", j0][:, ts, :].rearrange("p t (c i) -> p c t i", i=2),
                     ALU.add,
                 )
 
-        h_codes = {}
-        h_scales = {}
-
-        rounded = {}
-
-        def square_root(g, half, first, width):
-            rounded[g, half, first] = stage.tile([P, width, PACK], BF16, name="rounded", align_bytes=64, bufs=5)
+        def root_block(j0, width):
+            rounded[1, j0] = stage.tile([P, width, PACK], BF16, name="rounded1", align_bytes=64, bufs=3)
             nc.scalar.activation(
-                rounded[g, half, first][:].rearrange("p (c i) t -> p c i t", i=2),
-                power[g, half][:, first // 2 : (first + width) // 2].rearrange("p c u t i -> p c i (u t)"),
+                rounded[1, j0][:].rearrange("p (c i) t -> p c i t", i=2),
+                power[j0][:].rearrange("p c t i -> p c i t"),
                 ACT.Sqrt,
-            )
-
-        def quantize_envelope(g, half, first, width):
-            if first == 0:
-                h_codes[g, half] = keep.tile([P, HALF], U32, name="hc%d%d" % (g, half), align_bytes=64)
-                h_scales[g, half] = keep.tile([P, HALF], U8, name="hs%d%d" % (g, half), align_bytes=64)
-            cols = slice(first, first + width)
-            nc.vector.quantize_mx(
-                out=h_codes[g, half][:, cols].bitcast(E4M3),
-                scales=h_scales[g, half][:, cols],
-                in_=rounded[g, half, first][:].rearrange("p c t -> p (c t)"),
             )
 
         out_rows = out.rearrange("(c p) j -> p c j", p=P)
 
-        def cell_pass(acc, c, g, half, cols):
-            cells = slice(c * P, (c + 1) * P)
-            nc.tensor.matmul_mx(
-                out=acc,
-                lhsT=w3_codes[:, g, cells].bitcast(E4M3),
-                lhsT_scale=w3_planes[4 * g : P, cells],
-                rhs=h_codes[g, half][:, cols].bitcast(E4M3),
-                rhs_scale=h_scales[g, half][:, cols],
-                start=(g == 0),
-                stop=(g == 1),
+        def cells(j0, width, scalar_pairs, banks="turns"):
+            cols = slice(j0, j0 + width)
+            order = (0, 1) if banks == "sums" else (1, 0)
+            for pair in range(2):
+                acc = psum.tile([P, 2, width], F32, name=banks, bufs=BANKS)
+                for i in range(2):
+                    rows = slice((2 * pair + i) * P, (2 * pair + i + 1) * P)
+                    for g in order:
+                        nc.tensor.matmul_mx(
+                            out=acc[:, i, :],
+                            lhsT=w3_codes[:, g, rows].bitcast(E4M3),
+                            lhsT_scale=w3_planes[4 * g : P, rows],
+                            rhs=h_codes[g][:, cols].bitcast(E4M3),
+                            rhs_scale=h_scales[g][:, cols],
+                            start=(g == order[0]),
+                            stop=(g == order[1]),
+                        )
+                result = stage.tile([P, 2, width], F32, name="result", bufs=10)
+                if pair in scalar_pairs:
+                    for i in range(2):
+                        c = 2 * pair + i
+                        nc.scalar.activation(result[:, i, :], acc[:, i, :], ACT.Copy, scale=gain[:, c : c + 1])
+                else:
+                    spread = gain[:, 2 * pair : 2 * pair + 2].unsqueeze(2).to_broadcast([P, 2, width])
+                    nc.vector.tensor_tensor(result[:], acc[:], spread, ALU.mult)
+                nc.sync.dma_start(out=out_rows[:, 2 * pair : 2 * pair + 2, cols], in_=result[:])
+
+        gather_words(0, 0, S)
+        for a in range(2):
+            round_strip("r", 0, a, True)
+        quantize_strip("r", 0, 0)
+        opened = []
+        for q in range(QUARTERS):
+            acc = psum.tile([P, 2, STRIP], F32, name="sums", bufs=BANKS)
+            for i in range(2):
+                strip_pass(acc, "r", 0, 0, q, i, i == 0, False)
+            opened.append(acc)
+        gather_words(1, 0, S)
+        quantize_strip("r", 0, 1)
+        for q in range(QUARTERS):
+            for i in range(2):
+                strip_pass(opened[q], "r", 0, 1, q, i, False, i == 1)
+            square_strip(opened[q], "r", 0, q)
+
+        w3_codes = keep.tile([P, 2, N], U32, name="table0", align_bytes=64)
+        nc.sync.dma_start(
+            out=w3_codes[:].bitcast(I32), in_=w3_words.rearrange("a p c i -> p a (c i)").bitcast(I32)
+        )
+        w3_planes = keep.tile([P, N], U8, name="table1", align_bytes=64)
+        nc.gpsimd.memset(w3_planes[:].bitcast(I32), 0)
+        for q in range(4):
+            nc.sync.dma_start(
+                out=w3_planes[32 * q : 32 * q + 8, :].bitcast(I32),
+                in_=w3_scales[:, 4 * q : 4 * q + 4, :].bitcast(I32),
             )
+        gain = keep.tile([P, N // P], F32, name="first_strip0", align_bytes=64)
+        with nc.allow_non_contiguous_dma(reason="one value of illum for each partition"):
+            nc.sync.dma_start(out=gain[:], in_=illum.rearrange("(c p) -> p c", p=P))
 
-        def store_pair(result, pair, half, first):
-            j0 = half * HALF + first
-            nc.sync.dma_start(out=out_rows[:, 2 * pair : 2 * pair + 2, j0 : j0 + PIECE], in_=result[:])
+        for part, c0 in (("i", 0), ("r", STRIP), ("i", STRIP)):
+            prepare_strip(part, c0)
+            for q in range(QUARTERS):
+                strip_sums(part, c0, q)
+        add_strip(2, 0, STRIP, "after_strips")
+        for a in range(2):
+            quantize_block("r", a)
+        for q in range(TENSOR_QUARTERS):
+            turn_and_root(q)
+        for q in range(QUARTERS - 1):
+            block_sums("r", q * QUARTER, QUARTER)
+        for a in range(2):
+            quantize_block("i", a)
+        add_strip(2, STRIP, STRIP, None)
+        h_scales.insert(0, keep.tile([P, S], U8, name="after_block0", align_bytes=64))
+        add_strip(3, 0, PASS, "after_block1")
+        for q in range(2):
+            quantize_envelope(0, q * QUARTER, QUARTER)
 
-        def cells_two_to_a_bank(half, first):
-            cols = slice(first, first + PIECE)
-            for pair in range(2):
-                acc = psum.tile([P, 2, PIECE], F32, name="cells", bufs=2)
-                for i in range(2):
-                    for g in range(2):
-                        cell_pass(acc[:, i, :], 2 * pair + i, g, half, cols)
-                result = stage.tile([P, 2, PIECE], F32, name="result", bufs=8)
-                spread = gain[:, 2 * pair : 2 * pair + 2].unsqueeze(2).to_broadcast([P, 2, PIECE])
-                nc.vector.tensor_tensor(result[:], acc[:], spread, ALU.mult)
-                store_pair(result, pair, half, first)
-
-        def cells_one_to_a_bank(half, first, shared):
-            cols = slice(first, first + PIECE)
-            accs = [psum.tile([P, PIECE], F32, name="acc", bufs=6) for c in range(4)]
-            for c in range(4):
-                cell_pass(accs[c][:], c, 0, half, cols)
-            for pair in range(2):
-                result = stage.tile([P, 2, PIECE], F32, name="result", bufs=8)
-                for i in range(2):
-                    c = 2 * pair + i
-                    cell_pass(accs[c][:], c, 1, half, cols)
-                    if shared and i == 1:
-                        nc.scalar.activation(result[:, i, :], accs[c][:], ACT.Copy, scale=gain[:, c : c + 1])
-                    else:
-                        nc.vector.tensor_scalar(result[:, i, :], accs[c][:], gain[:, c : c + 1], None, ALU.mult)
-                store_pair(result, pair, half, first)
-
-        def envelope(g, half, first):
-            square_root(g, half, first, PIECE)
-            quantize_envelope(g, half, first, PIECE)
-
-        halves = [[(half, t) for t in range(PACK)] for half in range(2)]
-        both = halves[0] + halves[1]
-        by_pairs = [(half, 2 * u + i) for u in range(2) for half in range(2) for i in range(2)]
-
-        gather_words(0, 0)
-        quantize_weights("r", 0, 0, (0, 1))
-        gather_words(0, 1)
-        open_sums("r", 0, by_pairs[:4], 0)
-        gather_words(1, 0)
-        quantize_weights("r", 0, 1, (1,))
-        gather_words(1, 1)
-        close_sums("r", 0, by_pairs[:4], 1)
-        late_sums("r", 0, by_pairs[4:])
-
-        quantize_weights("i", 0, 0, ())
-        filter_stage("i", 0, both, 2)
-        add_squares(0, 0)
-        square_root(0, 0, 0, HALF)
-
-        quantize_weights("r", 1, 0, ())
-        filter_stage("r", 1, halves[0], 2)
-        quantize_weights("i", 1, 0, ())
-        quantize_weights("i", 1, 1, ())
-        quantize_envelope(0, 0, 0, HALF)
-        add_squares(0, 1)
-        late_sums("r", 1, halves[1])
-        late_sums("i", 1, halves[0])
-        add_squares(1, 0)
-        envelope(1, 0, 0)
-        late_sums("i", 1, halves[1])
-        add_squares(1, 1)
-        envelope(1, 0, PIECE)
-        for first in (0, PIECE):
-            cells_two_to_a_bank(0, first)
-        for first in (0, PIECE):
-            envelope(0, 1, first)
-            envelope(1, 1, first)
-        for first in (0, PIECE):
-            cells_one_to_a_bank(1, first, first > 0)
+        last = S - QUARTER
+        for q in range(QUARTERS - 1):
+            j0 = q * QUARTER
+            block_sums("i", j0, QUARTER)
+            add_block(j0, QUARTER)
+            if q < QUARTERS - TENSOR_QUARTERS:
+                turn_and_root(q + TENSOR_QUARTERS)
+            else:
+                block_sums("r", last, QUARTER)
+            if q > 0:
+                cells(j0 - QUARTER, QUARTER, ())
+            root_block(j0, QUARTER)
+            quantize_envelope(1, j0, QUARTER)
+            if q < QUARTERS - TENSOR_QUARTERS:
+                quantize_envelope(0, (q + TENSOR_QUARTERS) * QUARTER, QUARTER)
+        for j0 in (last, last + P):
+            block_sums("i", j0, P)
+            add_block(j0, P)
+        for j0 in (last, last + P):
+            root_block(j0, P)
+            quantize_envelope(1, j0, P)
+        cells(last - QUARTER, QUARTER, (1,))
+        for j0 in (last, last + P):
+            cells(j0, P, (1,), "sums")

@@ -24,7 +24,7 @@ QUARTER = 256
 QUARTERS = S // QUARTER
 STRIP = 256
 BANKS = 4
-TENSOR_QUARTERS = 2
+TENSOR_QUARTERS = 1
 
 
 def tile_list_residual_envelope_map_kernel(
@@ -165,9 +165,7 @@ def tile_list_residual_envelope_map_kernel(
 
         vector_sums = {}
 
-        def add_strip(q, c0, width, follows):
-            if c0 == 0:
-                vector_sums[q] = keep.tile([P, 2, PACK, P], F32, name=follows, align_bytes=64)
+        def add_strip(q, c0, width):
             ms = slice(c0 // PACK, (c0 + width) // PACK)
             nc.vector.tensor_tensor(
                 vector_sums[q][:, :, :, ms],
@@ -186,7 +184,7 @@ def tile_list_residual_envelope_map_kernel(
             if q < TENSOR_QUARTERS:
                 terms = [turned_squares["i", q][:], turned_squares["r", q][:]]
             else:
-                terms = [vector_sums[q][:]]
+                terms = [vector_sums[q]]
             for i in tiles:
                 turned = psum.tile([P, PACK, P], F32, name="turns", bufs=BANKS)
                 for t in range(PACK):
@@ -207,10 +205,11 @@ def tile_list_residual_envelope_map_kernel(
 
         def quantize_envelope(g, j0, width):
             cols = slice(j0, j0 + width)
+            first = j0 // QUARTER * QUARTER if g == 0 else j0
             nc.vector.quantize_mx(
                 out=h_codes[g][:, cols].bitcast(E4M3),
                 scales=h_scales[g][:, cols],
-                in_=rounded[g, j0][:].rearrange("p c t -> p (c t)"),
+                in_=rounded[g, first][:, j0 - first : j0 - first + width, :].rearrange("p c t -> p (c t)"),
             )
 
         def quantize_block(part, a):
@@ -258,7 +257,7 @@ def tile_list_residual_envelope_map_kernel(
         def close_bank(acc, part, j0, width, t0, a):
             per_bank = PASS // width
             if t0 == 0:
-                squares[part, j0] = stage.tile([P, PACK, width], F32, name="squares_" + part, bufs=3 if part == "r" else 2)
+                squares[part, j0] = stage.tile([P, PACK, width], F32, name="squares_" + part, bufs=3)
             for i in range(per_bank):
                 block_pass(acc[:, i, :], part, a, t0 + i, slice(j0, j0 + width), False, i == per_bank - 1)
             nc.scalar.activation(squares[part, j0][:, t0 : t0 + per_bank, :], acc[:], ACT.Square)
@@ -271,7 +270,10 @@ def tile_list_residual_envelope_map_kernel(
         power = {}
 
         def add_block(j0, width):
-            power[j0] = stage.tile([P, width // 2, PACK, 2], F32, name="power", bufs=2)
+            if j0 == 0:
+                power[j0] = keep.tile([P, width // 2, PACK, 2], F32, name="after_root")
+            else:
+                power[j0] = stage.tile([P, width // 2, PACK, 2], F32, name="power", bufs=2)
             per_bank = PASS // width
             q0 = j0 // QUARTER * QUARTER
             for t0 in range(0, PACK, per_bank):
@@ -298,19 +300,19 @@ def tile_list_residual_envelope_map_kernel(
             order = (0, 1) if banks == "sums" else (1, 0)
             for pair in range(2):
                 acc = psum.tile([P, 2, width], F32, name=banks, bufs=BANKS)
-                for i in range(2):
-                    rows = slice((2 * pair + i) * P, (2 * pair + i + 1) * P)
-                    for g in order:
+                for g in order:
+                    for i in range(2):
+                        rows = slice((2 * pair + i) * P, (2 * pair + i + 1) * P)
                         nc.tensor.matmul_mx(
                             out=acc[:, i, :],
                             lhsT=w3_codes[:, g, rows].bitcast(E4M3),
                             lhsT_scale=w3_planes[4 * g : P, rows],
                             rhs=h_codes[g][:, cols].bitcast(E4M3),
                             rhs_scale=h_scales[g][:, cols],
-                            start=(g == order[0]),
-                            stop=(g == order[1]),
+                            start=(g == order[0] and i == 0),
+                            stop=(g == order[1] and i == 1),
                         )
-                result = stage.tile([P, 2, width], F32, name="result", bufs=10)
+                result = stage.tile([P, 2, width], F32, name="result", bufs=7)
                 if pair in scalar_pairs:
                     for i in range(2):
                         c = 2 * pair + i
@@ -356,42 +358,65 @@ def tile_list_residual_envelope_map_kernel(
             prepare_strip(part, c0)
             for q in range(QUARTERS):
                 strip_sums(part, c0, q)
-        add_strip(2, 0, STRIP, "after_strips")
-        for a in range(2):
-            quantize_block("r", a)
-        for q in range(TENSOR_QUARTERS):
-            turn_and_root(q)
-        for q in range(QUARTERS - 1):
+        early_sums = keep.tile([P, 2, PACK, P], F32, name="after_strips", align_bytes=64)
+        vector_sums[1] = early_sums[:]
+        add_strip(1, 0, STRIP)
+        quantize_block("r", 0)
+        add_strip(1, STRIP, STRIP)
+        quantize_block("r", 1)
+        turn_and_root(0)
+        opened = [open_bank("r", 0, QUARTER, t0, 0) for t0 in (0, 2)]
+        turn_and_root(1)
+        for acc, t0 in zip(opened, (0, 2)):
+            close_bank(acc, "r", 0, QUARTER, t0, 1)
+        for q in range(1, QUARTERS - 1):
             block_sums("r", q * QUARTER, QUARTER)
         for a in range(2):
             quantize_block("i", a)
-        add_strip(2, STRIP, STRIP, None)
         h_scales.insert(0, keep.tile([P, S], U8, name="after_block0", align_bytes=64))
-        add_strip(3, 0, PASS, "after_block1")
-        for q in range(2):
-            quantize_envelope(0, q * QUARTER, QUARTER)
+        late_sums = keep.tile([P, 2, PACK, P], F32, name="after_block1", align_bytes=64)
+        vector_sums[2] = late_sums[:]
+        add_strip(2, 0, PASS)
 
-        last = S - QUARTER
-        for q in range(QUARTERS - 1):
-            j0 = q * QUARTER
+        for j0 in (0, QUARTER):
             block_sums("i", j0, QUARTER)
             add_block(j0, QUARTER)
-            if q < QUARTERS - TENSOR_QUARTERS:
-                turn_and_root(q + TENSOR_QUARTERS)
-            else:
-                block_sums("r", last, QUARTER)
-            if q > 0:
-                cells(j0 - QUARTER, QUARTER, ())
+        for j0 in (0, QUARTER):
+            quantize_envelope(0, j0, QUARTER)
             root_block(j0, QUARTER)
             quantize_envelope(1, j0, QUARTER)
-            if q < QUARTERS - TENSOR_QUARTERS:
-                quantize_envelope(0, (q + TENSOR_QUARTERS) * QUARTER, QUARTER)
-        for j0 in (last, last + P):
+        turn_and_root(2)
+        cells(0, QUARTER, ())
+        quantize_envelope(0, 2 * QUARTER, QUARTER)
+
+        last = S - QUARTER
+        units = list(range(S // 2, S, P))
+
+        def sums_and_add(j0):
             block_sums("i", j0, P)
             add_block(j0, P)
-        for j0 in (last, last + P):
+
+        def envelope(j0):
             root_block(j0, P)
             quantize_envelope(1, j0, P)
-        cells(last - QUARTER, QUARTER, (1,))
-        for j0 in (last, last + P):
+
+        for j0 in units[:2]:
+            sums_and_add(j0)
+        cells(QUARTER, QUARTER, ())
+        last_sums = keep.tile([P, 2, PACK, P], F32, name="after_root")
+        vector_sums[3] = last_sums[:]
+        add_strip(3, 0, PASS)
+        for i in range(2):
+            close_bank(open_bank("r", last, QUARTER, 2 * i, 1), "r", last, QUARTER, 2 * i, 0)
+            envelope(units[i])
+        for i in range(2):
+            sums_and_add(units[2 + i])
+            turn_and_root(3, (i,))
+            quantize_envelope(0, units[2 + i], P)
+            if i == 0:
+                cells(units[0], P, ())
+        for j0 in units[2:]:
+            envelope(j0)
+        cells(units[1], P, ())
+        for j0 in units[2:]:
             cells(j0, P, (1,), "sums")

@@ -100,37 +100,31 @@ def tile_list_residual_envelope_map_kernel(
         w_scales = {}
         grouped = {}
 
-        def round_strip(part, c0, a, on_scalar):
-            for u in range(2):
-                key = (part, c0, a, u)
-                if key == ("i", STRIP, 1, 1):
-                    grouped[key] = keep.tile([P, P * PACK], BF16, name="after_strips", align_bytes=64)
-                else:
-                    name = "strip_by_scalar" if on_scalar else "strip_by_vector"
-                    grouped[key] = stage.tile([P, P * PACK], BF16, name=name, align_bytes=64, bufs=4)
-                target = grouped[key][:].rearrange("p (c i j) -> p c j i", i=4, j=PACK)
-                source = raw[part, c0, a][:, :, u * P : (u + 1) * P].rearrange("p j (c i) -> p c j i", i=4)
-                if on_scalar:
-                    nc.scalar.copy(target, source)
-                else:
-                    nc.vector.tensor_copy(target, source)
+        def round_strip(part, c0, a, target, on_scalar):
+            target = target.rearrange("p (c i j) -> p c j i", i=4, j=PACK)
+            source = raw[part, c0, a].rearrange("p j (c i) -> p c j i", i=4)
+            if on_scalar:
+                nc.scalar.copy(target, source)
+            else:
+                nc.vector.tensor_copy(target, source)
 
-        def quantize_strip(part, c0, a):
-            key = (part, c0, a)
-            w_codes[key] = keep.tile([P, STRIP], U32, name="wc_%s%d_%d" % key, align_bytes=64)
-            w_scales[key] = keep.tile([P, STRIP], U8, name="ws_%s%d_%d" % key, align_bytes=64)
-            for u in range(2):
-                cols = slice(u * P, (u + 1) * P)
-                nc.vector.quantize_mx(
-                    out=w_codes[key][:, cols].bitcast(E4M3),
-                    scales=w_scales[key][:, cols],
-                    in_=grouped[part, c0, a, u][:],
-                )
+        def quantize_strip(part, c0, passes, source):
+            name = "%s%d_%d" % (part, c0, passes[0])
+            codes = keep.tile([P, len(passes) * STRIP], U32, name="wc_" + name, align_bytes=64)
+            planes = keep.tile([P, len(passes) * STRIP], U8, name="ws_" + name, align_bytes=64)
+            nc.vector.quantize_mx(out=codes[:].bitcast(E4M3), scales=planes[:], in_=source)
+            for n, a in enumerate(passes):
+                w_codes[part, c0, a] = codes[:, n * STRIP : (n + 1) * STRIP]
+                w_scales[part, c0, a] = planes[:, n * STRIP : (n + 1) * STRIP]
 
-        def prepare_strip(part, c0):
+        def prepare_strip(part, c0, scalar_passes):
+            if (part, c0) == ("i", STRIP):
+                both = keep.tile([P, 2, STRIP * PACK], BF16, name="after_strips", align_bytes=64)
+            else:
+                both = stage.tile([P, 2, STRIP * PACK], BF16, name="rounded_strip", align_bytes=64, bufs=2)
             for a in range(2):
-                round_strip(part, c0, a, False)
-                quantize_strip(part, c0, a)
+                round_strip(part, c0, a, both[:, a, :], a in scalar_passes)
+            quantize_strip(part, c0, (0, 1), both[:].rearrange("p a x -> p (a x)"))
 
         def strip_pass(acc, part, c0, a, q, i, start, stop):
             cols = slice(q * QUARTER + i * P, q * QUARTER + (i + 1) * P)
@@ -138,8 +132,8 @@ def tile_list_residual_envelope_map_kernel(
                 out=acc[:, i, :],
                 lhsT=v_codes[a][:, cols].bitcast(E5M2),
                 lhsT_scale=v_scales[a][:, cols],
-                rhs=w_codes[part, c0, a][:].bitcast(E4M3),
-                rhs_scale=w_scales[part, c0, a][:],
+                rhs=w_codes[part, c0, a].bitcast(E4M3),
+                rhs_scale=w_scales[part, c0, a],
                 start=start,
                 stop=stop,
             )
@@ -295,14 +289,14 @@ def tile_list_residual_envelope_map_kernel(
 
         out_rows = out.rearrange("(c p) j -> p c j", p=P)
 
-        def cells(j0, width, scalar_pairs, banks="turns"):
+        def cells(j0, width, per_bank, shared):
             cols = slice(j0, j0 + width)
-            order = (0, 1) if banks == "sums" else (1, 0)
-            for pair in range(2):
-                acc = psum.tile([P, 2, width], F32, name=banks, bufs=BANKS)
+            order = (0, 1) if shared else (1, 0)
+            for c0 in range(0, N // P, per_bank):
+                acc = psum.tile([P, per_bank, width], F32, name="sums" if shared else "turns", bufs=BANKS)
                 for g in order:
-                    for i in range(2):
-                        rows = slice((2 * pair + i) * P, (2 * pair + i + 1) * P)
+                    for i in range(per_bank):
+                        rows = slice((c0 + i) * P, (c0 + i + 1) * P)
                         nc.tensor.matmul_mx(
                             out=acc[:, i, :],
                             lhsT=w3_codes[:, g, rows].bitcast(E4M3),
@@ -310,22 +304,24 @@ def tile_list_residual_envelope_map_kernel(
                             rhs=h_codes[g][:, cols].bitcast(E4M3),
                             rhs_scale=h_scales[g][:, cols],
                             start=(g == order[0] and i == 0),
-                            stop=(g == order[1] and i == 1),
+                            stop=(g == order[1] and i == per_bank - 1),
                         )
-                result = stage.tile([P, 2, width], F32, name="result", bufs=7)
-                if pair in scalar_pairs:
-                    for i in range(2):
-                        c = 2 * pair + i
-                        nc.scalar.activation(result[:, i, :], acc[:, i, :], ACT.Copy, scale=gain[:, c : c + 1])
+                name = "last_results" if shared else "results"
+                result = stage.tile([P, per_bank, width], F32, name=name, bufs=4)
+                if shared and c0 > 0:
+                    for i in range(per_bank):
+                        factor = gain[:, c0 + i : c0 + i + 1]
+                        nc.scalar.activation(result[:, i, :], acc[:, i, :], ACT.Copy, scale=factor)
                 else:
-                    spread = gain[:, 2 * pair : 2 * pair + 2].unsqueeze(2).to_broadcast([P, 2, width])
+                    spread = gain[:, c0 : c0 + per_bank].unsqueeze(2).to_broadcast([P, per_bank, width])
                     nc.vector.tensor_tensor(result[:], acc[:], spread, ALU.mult)
-                nc.sync.dma_start(out=out_rows[:, 2 * pair : 2 * pair + 2, cols], in_=result[:])
+                nc.sync.dma_start(out=out_rows[:, c0 : c0 + per_bank, cols], in_=result[:])
 
         gather_words(0, 0, S)
         for a in range(2):
-            round_strip("r", 0, a, True)
-        quantize_strip("r", 0, 0)
+            grouped[a] = keep.tile([P, STRIP * PACK], BF16, name="first_rounded%d" % a, align_bytes=64)
+            round_strip("r", 0, a, grouped[a][:], True)
+        quantize_strip("r", 0, (0,), grouped[0][:])
         opened = []
         for q in range(QUARTERS):
             acc = psum.tile([P, 2, STRIP], F32, name="sums", bufs=BANKS)
@@ -333,7 +329,7 @@ def tile_list_residual_envelope_map_kernel(
                 strip_pass(acc, "r", 0, 0, q, i, i == 0, False)
             opened.append(acc)
         gather_words(1, 0, S)
-        quantize_strip("r", 0, 1)
+        quantize_strip("r", 0, (1,), grouped[1][:])
         for q in range(QUARTERS):
             for i in range(2):
                 strip_pass(opened[q], "r", 0, 1, q, i, False, i == 1)
@@ -355,7 +351,7 @@ def tile_list_residual_envelope_map_kernel(
             nc.sync.dma_start(out=gain[:], in_=illum.rearrange("(c p) -> p c", p=P))
 
         for part, c0 in (("i", 0), ("r", STRIP), ("i", STRIP)):
-            prepare_strip(part, c0)
+            prepare_strip(part, c0, (0,) if c0 == 0 else ())
             for q in range(QUARTERS):
                 strip_sums(part, c0, q)
         early_sums = keep.tile([P, 2, PACK, P], F32, name="after_strips", align_bytes=64)
@@ -386,7 +382,7 @@ def tile_list_residual_envelope_map_kernel(
             root_block(j0, QUARTER)
             quantize_envelope(1, j0, QUARTER)
         turn_and_root(2)
-        cells(0, QUARTER, ())
+        cells(0, QUARTER, 2, False)
         quantize_envelope(0, 2 * QUARTER, QUARTER)
 
         last = S - QUARTER
@@ -402,7 +398,7 @@ def tile_list_residual_envelope_map_kernel(
 
         for j0 in units[:2]:
             sums_and_add(j0)
-        cells(QUARTER, QUARTER, ())
+        cells(QUARTER, QUARTER, 2, False)
         last_sums = keep.tile([P, 2, PACK, P], F32, name="after_root")
         vector_sums[3] = last_sums[:]
         add_strip(3, 0, PASS)
@@ -414,9 +410,9 @@ def tile_list_residual_envelope_map_kernel(
             turn_and_root(3, (i,))
             quantize_envelope(0, units[2 + i], P)
             if i == 0:
-                cells(units[0], P, ())
+                cells(units[0], P, 4, False)
         for j0 in units[2:]:
             envelope(j0)
-        cells(units[1], P, ())
+        cells(units[1], P, 4, False)
         for j0 in units[2:]:
-            cells(j0, P, (1,), "sums")
+            cells(j0, P, 2, True)

@@ -216,7 +216,7 @@ def tile_list_residual_envelope_map_kernel(
                 if (part, a) == ("i", 1):
                     pair = keep.tile([P, 2, P, PACK], BF16, name="after_block%d" % u, align_bytes=64)
                 else:
-                    pair = stage.tile([P, 2, P, PACK], BF16, name="block_pair", align_bytes=64, bufs=2)
+                    pair = stage.tile([P, 2, P, PACK], BF16, name="block_pair", align_bytes=64, bufs=3)
                 nc.vector.tensor_copy(pair[:].rearrange("p t m j -> p m j t"), source[:, :, :, 2 * u : 2 * u + 2])
                 pairs.append(pair)
             for u in range(2):
@@ -251,7 +251,8 @@ def tile_list_residual_envelope_map_kernel(
         def close_bank(acc, part, j0, width, t0, a):
             per_bank = PASS // width
             if t0 == 0:
-                squares[part, j0] = stage.tile([P, PACK, width], F32, name="squares_" + part, bufs=3)
+                held = keep.tile([P, PACK, width], F32, name="squares_%s%d" % (part, j0))
+                squares[part, j0] = held[:]
             for i in range(per_bank):
                 block_pass(acc[:, i, :], part, a, t0 + i, slice(j0, j0 + width), False, i == per_bank - 1)
             nc.scalar.activation(squares[part, j0][:, t0 : t0 + per_bank, :], acc[:], ACT.Square)
@@ -280,7 +281,7 @@ def tile_list_residual_envelope_map_kernel(
                 )
 
         def root_block(j0, width):
-            rounded[1, j0] = stage.tile([P, width, PACK], BF16, name="rounded1", align_bytes=64, bufs=3)
+            rounded[1, j0] = keep.tile([P, width, PACK], BF16, name="rounded1_%d" % j0, align_bytes=64)
             nc.scalar.activation(
                 rounded[1, j0][:].rearrange("p (c i) t -> p c i t", i=2),
                 power[j0][:].rearrange("p c t i -> p c i t"),
@@ -289,7 +290,7 @@ def tile_list_residual_envelope_map_kernel(
 
         out_rows = out.rearrange("(c p) j -> p c j", p=P)
 
-        def cells(j0, width, per_bank, shared):
+        def cells(j0, width, per_bank, shared, by_scalar=()):
             cols = slice(j0, j0 + width)
             order = (0, 1) if shared else (1, 0)
             for c0 in range(0, N // P, per_bank):
@@ -306,16 +307,20 @@ def tile_list_residual_envelope_map_kernel(
                             start=(g == order[0] and i == 0),
                             stop=(g == order[1] and i == per_bank - 1),
                         )
-                name = "last_results" if shared else "results"
-                result = stage.tile([P, per_bank, width], F32, name=name, bufs=4)
-                if shared and c0 > 0:
+                if c0 in by_scalar:
+                    held = keep.tile([P, per_bank, width], F32, name="first_strip1" if per_bank == 4 else "first_rounded0", align_bytes=64)
+                    result = held[:]
+                else:
+                    first = N // P * j0 + c0 * width
+                    result = landing[:, first : first + per_bank * width].rearrange("p (i c) -> p i c", i=per_bank)
+                if c0 in by_scalar:
                     for i in range(per_bank):
                         factor = gain[:, c0 + i : c0 + i + 1]
                         nc.scalar.activation(result[:, i, :], acc[:, i, :], ACT.Copy, scale=factor)
                 else:
                     spread = gain[:, c0 : c0 + per_bank].unsqueeze(2).to_broadcast([P, per_bank, width])
-                    nc.vector.tensor_tensor(result[:], acc[:], spread, ALU.mult)
-                nc.sync.dma_start(out=out_rows[:, c0 : c0 + per_bank, cols], in_=result[:])
+                    nc.vector.tensor_tensor(result, acc[:], spread, ALU.mult)
+                nc.sync.dma_start(out=out_rows[:, c0 : c0 + per_bank, cols], in_=result)
 
         gather_words(0, 0, S)
         for a in range(2):
@@ -339,7 +344,7 @@ def tile_list_residual_envelope_map_kernel(
         nc.sync.dma_start(
             out=w3_codes[:].bitcast(I32), in_=w3_words.rearrange("a p c i -> p a (c i)").bitcast(I32)
         )
-        w3_planes = keep.tile([P, N], U8, name="table1", align_bytes=64)
+        w3_planes = keep.tile([P, N], U8, name="first_rounded1", align_bytes=64)
         nc.gpsimd.memset(w3_planes[:].bitcast(I32), 0)
         for q in range(4):
             nc.sync.dma_start(
@@ -414,5 +419,5 @@ def tile_list_residual_envelope_map_kernel(
         for j0 in units[2:]:
             envelope(j0)
         cells(units[1], P, 4, False)
-        for j0 in units[2:]:
-            cells(j0, P, 2, True)
+        cells(units[2], P, 4, True, (0,))
+        cells(units[3], P, 2, True, (2,))

@@ -124,7 +124,8 @@ def tile_list_residual_envelope_map_kernel(
                 both = stage.tile([P, 2, STRIP * PACK], BF16, name="rounded_strip", align_bytes=64, bufs=2)
             for a in range(2):
                 round_strip(part, c0, a, both[:, a, :], a in scalar_passes)
-            quantize_strip(part, c0, (0, 1), both[:].rearrange("p a x -> p (a x)"))
+            for a in range(2):
+                quantize_strip(part, c0, (a,), both[:, a, :])
 
         def strip_pass(acc, part, c0, a, q, i, start, stop):
             cols = slice(q * QUARTER + i * P, q * QUARTER + (i + 1) * P)
@@ -152,9 +153,10 @@ def tile_list_residual_envelope_map_kernel(
 
         def strip_sums(part, c0, q):
             acc = psum.tile([P, 2, STRIP], F32, name="sums", bufs=BANKS)
-            for i in range(2):
-                for a in (1, 0):
-                    strip_pass(acc, part, c0, a, q, i, a == 1, a == 0)
+            order = (0, 1) if q == 0 else (1, 0)
+            for a in order:
+                for i in range(2):
+                    strip_pass(acc, part, c0, a, q, i, (a, i) == (order[0], 0), (a, i) == (order[1], 1))
             square_strip(acc, part, c0, q)
 
         vector_sums = {}

@@ -359,7 +359,7 @@ def tile_list_residual_envelope_map_kernel(
 
         for part, c0 in (("i", 0), ("r", STRIP), ("i", STRIP)):
             prepare_strip(part, c0, (0,) if c0 == 0 else ())
-            for q in range(QUARTERS):
+            for q in range(QUARTERS - 1 if (part, c0) == ("i", STRIP) else QUARTERS):
                 strip_sums(part, c0, q)
         early_sums = keep.tile([P, 2, PACK, P], F32, name="after_strips", align_bytes=64)
         vector_sums[1] = early_sums[:]
@@ -368,12 +368,12 @@ def tile_list_residual_envelope_map_kernel(
         add_strip(1, STRIP, STRIP)
         quantize_block("r", 1)
         turn_and_root(0)
-        opened = [open_bank("r", 0, QUARTER, t0, 0) for t0 in (0, 2)]
+        strip_sums("i", STRIP, QUARTERS - 1)
         turn_and_root(1)
-        for acc, t0 in zip(opened, (0, 2)):
-            close_bank(acc, "r", 0, QUARTER, t0, 1)
-        for q in range(1, QUARTERS - 1):
+        for q in range(QUARTERS - 1):
             block_sums("r", q * QUARTER, QUARTER)
+        last = S - QUARTER
+        close_bank(open_bank("r", last, QUARTER, 0, 1), "r", last, QUARTER, 0, 0)
         for a in range(2):
             quantize_block("i", a)
         h_scales.insert(0, keep.tile([P, S], U8, name="after_block0", align_bytes=64))
@@ -392,7 +392,6 @@ def tile_list_residual_envelope_map_kernel(
         cells(0, QUARTER, 2, False)
         quantize_envelope(0, 2 * QUARTER, QUARTER)
 
-        last = S - QUARTER
         units = list(range(S // 2, S, P))
 
         def sums_and_add(j0):
@@ -409,9 +408,9 @@ def tile_list_residual_envelope_map_kernel(
         last_sums = keep.tile([P, 2, PACK, P], F32, name="after_root")
         vector_sums[3] = last_sums[:]
         add_strip(3, 0, PASS)
-        for i in range(2):
-            close_bank(open_bank("r", last, QUARTER, 2 * i, 1), "r", last, QUARTER, 2 * i, 0)
-            envelope(units[i])
+        close_bank(open_bank("r", last, QUARTER, 2, 1), "r", last, QUARTER, 2, 0)
+        for j0 in units[:2]:
+            envelope(j0)
         for i in range(2):
             sums_and_add(units[2 + i])
             turn_and_root(3, (i,))

@@ -83,12 +83,20 @@ def tile_list_residual_envelope_map_kernel(
         v_scales = [picked_scales, moved_scales]
 
         late = [("i", 0, STRIP), ("r", STRIP, STRIP), ("i", STRIP, STRIP), ("r", PASS, PASS), ("i", PASS, PASS)]
-        landing = keep.tile([P, sum(2 * PACK * w for part, c0, w in late)], F32, name="late_loads", align_bytes=64)
-        at = 0
-        for part, c0, width in late:
-            for a in range(2):
-                load_weights(landing[:, at : at + PACK * width], part, c0, width, a)
-                at = at + PACK * width
+        apart = {("r", STRIP, 1): "table0", ("i", STRIP, 1): "first_strip0"}
+        pieces = [(part, c0, width, a) for part, c0, width in late for a in range(2)]
+        shared = [piece for piece in pieces if (piece[0], piece[1], piece[3]) not in apart]
+        landing = keep.tile([P, sum(PACK * piece[2] for piece in shared)], F32, name="late_loads", align_bytes=64)
+
+        def load_late():
+            at = 0
+            for part, c0, width, a in pieces:
+                if (part, c0, a) in apart:
+                    own = keep.tile([P, PACK * width], F32, name=apart[part, c0, a], align_bytes=64)
+                    load_weights(own[:], part, c0, width, a)
+                else:
+                    load_weights(landing[:, at : at + PACK * width], part, c0, width, a)
+                    at = at + PACK * width
 
         v_codes = [keep.tile([P, S], U32, name="v_codes%d" % a, align_bytes=64) for a in range(2)]
 
@@ -110,7 +118,8 @@ def tile_list_residual_envelope_map_kernel(
 
         def quantize_strip(part, c0, passes, source):
             name = "%s%d_%d" % (part, c0, passes[0])
-            codes = keep.tile([P, len(passes) * STRIP], U32, name="wc_" + name, align_bytes=64)
+            behind = apart.get((part, c0, passes[0] + 1), "wc_" + name)
+            codes = keep.tile([P, len(passes) * STRIP], U32, name=behind, align_bytes=64)
             planes = keep.tile([P, len(passes) * STRIP], U8, name="ws_" + name, align_bytes=64)
             nc.vector.quantize_mx(out=codes[:].bitcast(E4M3), scales=planes[:], in_=source)
             for n, a in enumerate(passes):
@@ -310,7 +319,7 @@ def tile_list_residual_envelope_map_kernel(
                             stop=(g == order[1] and i == per_bank - 1),
                         )
                 if c0 in by_scalar:
-                    held = keep.tile([P, per_bank, width], F32, name="first_strip1" if per_bank == 4 else "first_rounded0", align_bytes=64)
+                    held = keep.tile([P, per_bank, width], F32, name="scaled" if per_bank == 4 else "first_rounded0", align_bytes=64)
                     result = held[:]
                 else:
                     first = N // P * j0 + c0 * width
@@ -328,6 +337,7 @@ def tile_list_residual_envelope_map_kernel(
         for a in range(2):
             grouped[a] = keep.tile([P, STRIP * PACK], BF16, name="first_rounded%d" % a, align_bytes=64)
             round_strip("r", 0, a, grouped[a][:], True)
+        load_late()
         quantize_strip("r", 0, (0,), grouped[0][:])
         opened = []
         for q in range(QUARTERS):
@@ -342,7 +352,7 @@ def tile_list_residual_envelope_map_kernel(
                 strip_pass(opened[q], "r", 0, 1, q, i, False, i == 1)
             square_strip(opened[q], "r", 0, q)
 
-        w3_codes = keep.tile([P, 2, N], U32, name="table0", align_bytes=64)
+        w3_codes = keep.tile([P, 2, N], U32, name="table1", align_bytes=64)
         nc.sync.dma_start(
             out=w3_codes[:].bitcast(I32), in_=w3_words.rearrange("a p c i -> p a (c i)").bitcast(I32)
         )
@@ -353,7 +363,7 @@ def tile_list_residual_envelope_map_kernel(
                 out=w3_planes[32 * q : 32 * q + 8, :].bitcast(I32),
                 in_=w3_scales[:, 4 * q : 4 * q + 4, :].bitcast(I32),
             )
-        gain = keep.tile([P, N // P], F32, name="first_strip0", align_bytes=64)
+        gain = keep.tile([P, N // P], F32, name="first_strip1", align_bytes=64)
         with nc.allow_non_contiguous_dma(reason="one value of illum for each partition"):
             nc.sync.dma_start(out=gain[:], in_=illum.rearrange("(c p) -> p c", p=P))
 

@@ -23,8 +23,6 @@ PASS = P * PACK
 QUARTER = 256
 QUARTERS = S // QUARTER
 STRIP = 256
-BANKS = 4
-TENSOR_QUARTERS = 1
 
 
 def tile_list_residual_envelope_map_kernel(
@@ -33,8 +31,10 @@ def tile_list_residual_envelope_map_kernel(
     nc = tc.nc
     with ExitStack() as ctx:
         keep = ctx.enter_context(tc.tile_pool(name="keep", bufs=1))
-        stage = ctx.enter_context(tc.tile_pool(name="stage", bufs=2))
         psum = ctx.enter_context(tc.psum_pool(name="psum", bufs=1))
+
+        def in_bank(bank, shape):
+            return psum.tile(shape, F32, name="bank%d" % bank)
 
         offsets = keep.tile([P, S // 16], U16, name="offsets")
         nc.sync.dma_start(offsets[:], offs)
@@ -83,20 +83,12 @@ def tile_list_residual_envelope_map_kernel(
         v_scales = [picked_scales, moved_scales]
 
         late = [("i", 0, STRIP), ("r", STRIP, STRIP), ("i", STRIP, STRIP), ("r", PASS, PASS), ("i", PASS, PASS)]
-        apart = {("r", STRIP, 1): "table0", ("i", STRIP, 1): "first_strip0"}
-        pieces = [(part, c0, width, a) for part, c0, width in late for a in range(2)]
-        shared = [piece for piece in pieces if (piece[0], piece[1], piece[3]) not in apart]
-        landing = keep.tile([P, sum(PACK * piece[2] for piece in shared)], F32, name="late_loads", align_bytes=64)
-
-        def load_late():
-            at = 0
-            for part, c0, width, a in pieces:
-                if (part, c0, a) in apart:
-                    own = keep.tile([P, PACK * width], F32, name=apart[part, c0, a], align_bytes=64)
-                    load_weights(own[:], part, c0, width, a)
-                else:
-                    load_weights(landing[:, at : at + PACK * width], part, c0, width, a)
-                    at = at + PACK * width
+        landing = keep.tile([P, sum(2 * PACK * piece[2] for piece in late)], F32, name="late_loads", align_bytes=64)
+        at = 0
+        for part, c0, width in late:
+            for a in range(2):
+                load_weights(landing[:, at : at + PACK * width], part, c0, width, a)
+                at = at + PACK * width
 
         v_codes = [keep.tile([P, S], U32, name="v_codes%d" % a, align_bytes=64) for a in range(2)]
 
@@ -108,249 +100,205 @@ def tile_list_residual_envelope_map_kernel(
         w_scales = {}
         grouped = {}
 
-        def round_strip(part, c0, a, target, on_scalar):
+        def round_strip(part, c0, a, target, scalar_columns):
+            grouped[part, c0, a] = target
             target = target.rearrange("p (c i j) -> p c j i", i=4, j=PACK)
             source = raw[part, c0, a].rearrange("p j (c i) -> p c j i", i=4)
-            if on_scalar:
-                nc.scalar.copy(target, source)
-            else:
-                nc.vector.tensor_copy(target, source)
+            cut = scalar_columns // 4
+            if scalar_columns > 0:
+                nc.scalar.copy(target[:, :cut], source[:, :cut])
+            if scalar_columns < STRIP:
+                nc.vector.tensor_copy(target[:, cut:], source[:, cut:])
 
-        def quantize_strip(part, c0, passes, source):
-            name = "%s%d_%d" % (part, c0, passes[0])
-            behind = apart.get((part, c0, passes[0] + 1), "wc_" + name)
-            codes = keep.tile([P, len(passes) * STRIP], U32, name=behind, align_bytes=64)
-            planes = keep.tile([P, len(passes) * STRIP], U8, name="ws_" + name, align_bytes=64)
-            nc.vector.quantize_mx(out=codes[:].bitcast(E4M3), scales=planes[:], in_=source)
-            for n, a in enumerate(passes):
-                w_codes[part, c0, a] = codes[:, n * STRIP : (n + 1) * STRIP]
-                w_scales[part, c0, a] = planes[:, n * STRIP : (n + 1) * STRIP]
+        def quantize_strip(part, c0, a):
+            key = (part, c0, a)
+            codes = keep.tile([P, STRIP], U32, name="wc_%s%d_%d" % key, align_bytes=64)
+            planes = keep.tile([P, STRIP], U8, name="ws_%s%d_%d" % key, align_bytes=64)
+            nc.vector.quantize_mx(out=codes[:].bitcast(E4M3), scales=planes[:], in_=grouped[key])
+            w_codes[key] = codes[:]
+            w_scales[key] = planes[:]
 
-        def prepare_strip(part, c0, scalar_passes):
-            if (part, c0) == ("i", STRIP):
-                both = keep.tile([P, 2, STRIP * PACK], BF16, name="after_strips", align_bytes=64)
-            else:
-                both = stage.tile([P, 2, STRIP * PACK], BF16, name="rounded_strip", align_bytes=64, bufs=2)
-            for a in range(2):
-                round_strip(part, c0, a, both[:, a, :], a in scalar_passes)
-            for a in range(2):
-                quantize_strip(part, c0, (a,), both[:, a, :])
+        def strip_pass(acc, part, c0, a, q, first):
+            for i in range(2):
+                cols = slice(q * QUARTER + i * P, q * QUARTER + (i + 1) * P)
+                nc.tensor.matmul_mx(
+                    out=acc[:, i, :],
+                    lhsT=v_codes[a][:, cols].bitcast(E5M2),
+                    lhsT_scale=v_scales[a][:, cols],
+                    rhs=w_codes[part, c0, a].bitcast(E4M3),
+                    rhs_scale=w_scales[part, c0, a],
+                    start=(a == first and i == 0),
+                    stop=(a != first and i == 1),
+                )
 
-        def strip_pass(acc, part, c0, a, q, i, start, stop):
-            cols = slice(q * QUARTER + i * P, q * QUARTER + (i + 1) * P)
-            nc.tensor.matmul_mx(
-                out=acc[:, i, :],
-                lhsT=v_codes[a][:, cols].bitcast(E5M2),
-                lhsT_scale=v_scales[a][:, cols],
-                rhs=w_codes[part, c0, a].bitcast(E4M3),
-                rhs_scale=w_scales[part, c0, a],
-                start=start,
-                stop=stop,
-            )
-
-        turned_squares = {}
+        strip_squares = {}
 
         def square_strip(acc, part, c0, q):
-            if (part, q) not in turned_squares:
-                turned_squares[part, q] = keep.tile([P, 2, PACK, P], F32, name="turned_%s%d" % (part, q))
+            if (part, q) not in strip_squares:
+                strip_squares[part, q] = keep.tile([P, 2, PACK, P], F32, name="strip_squares_%s%d" % (part, q))
             m0 = c0 // PACK
             nc.scalar.activation(
-                turned_squares[part, q][:, :, :, m0 : m0 + STRIP // PACK],
+                strip_squares[part, q][:, :, :, m0 : m0 + STRIP // PACK],
                 acc[:].rearrange("p i (m t) -> p i t m", t=PACK),
                 ACT.Square,
             )
 
-        def strip_sums(part, c0, q):
-            acc = psum.tile([P, 2, STRIP], F32, name="sums", bufs=BANKS)
-            order = (0, 1) if q == 0 else (1, 0)
-            for a in order:
-                for i in range(2):
-                    strip_pass(acc, part, c0, a, q, i, (a, i) == (order[0], 0), (a, i) == (order[1], 1))
+        def strip_sums(part, c0, q, bank):
+            acc = in_bank(bank, [P, 2, STRIP])
+            first = 0 if q == 0 or (part, c0) == ("r", 0) else 1
+            for a in (first, 1 - first):
+                strip_pass(acc, part, c0, a, q, first)
             square_strip(acc, part, c0, q)
 
-        vector_sums = {}
+        strip_power = {}
 
-        def add_strip(q, c0, width):
-            ms = slice(c0 // PACK, (c0 + width) // PACK)
+        def add_strip(q, i, ms, target):
             nc.vector.tensor_tensor(
-                vector_sums[q][:, :, :, ms],
-                turned_squares["r", q][:, :, :, ms],
-                turned_squares["i", q][:, :, :, ms],
-                ALU.add,
+                target, strip_squares["r", q][:, i, :, ms], strip_squares["i", q][:, i, :, ms], ALU.add
             )
 
-        rounded = {}
-        h_codes = [keep.tile([P, S], U32, name="h_codes%d" % g, align_bytes=64) for g in range(2)]
-        h_scales = [keep.tile([P, S], U8, name="h_scales1", align_bytes=64)]
+        def add_tile(q, i, spent):
+            strip_power[q, i] = keep.tile([P, PACK, P], F32, name=spent, align_bytes=64)[:]
+            add_strip(q, i, slice(0, P), strip_power[q, i])
 
-        def turn_and_root(q, tiles=(0, 1)):
-            if 0 in tiles:
-                rounded[0, q * QUARTER] = stage.tile([P, QUARTER, PACK], BF16, name="rounded0", align_bytes=64, bufs=2)
-            if q < TENSOR_QUARTERS:
-                terms = [turned_squares["i", q][:], turned_squares["r", q][:]]
+        rounded = {}
+
+        def hold_envelope(g, j0, width, name):
+            held = keep.tile([P, width, PACK], BF16, name=name, align_bytes=64)
+            for tile in range(j0 // P, (j0 + width) // P):
+                rounded[g, tile] = (j0, held)
+
+        h_codes = [keep.tile([P, S], U32, name="h_codes%d" % g, align_bytes=64) for g in range(2)]
+        h_scales = {1: keep.tile([P, S], U8, name="h_scales1", align_bytes=64)}
+
+        def turn_and_root(q, i, bank):
+            j0 = q * QUARTER + i * P
+            if (q, i) in strip_power:
+                terms = [strip_power[q, i]]
             else:
-                terms = [vector_sums[q]]
-            for i in tiles:
-                turned = psum.tile([P, PACK, P], F32, name="turns", bufs=BANKS)
-                for t in range(PACK):
-                    for n, term in enumerate(terms):
-                        nc.tensor.matmul(
-                            turned[:, t, :],
-                            term[:, i, t, :],
-                            identity[:],
-                            start=(n == 0),
-                            stop=(n == len(terms) - 1),
-                            is_transpose=True,
-                        )
-                nc.scalar.activation(
-                    rounded[0, q * QUARTER][:, i * P : (i + 1) * P, :],
-                    turned[:].rearrange("p t j -> p j t"),
-                    ACT.Sqrt,
-                )
+                terms = [strip_squares["i", q][:, i], strip_squares["r", q][:, i]]
+            turned = in_bank(bank, [P, PACK, P])
+            for t in range(PACK):
+                for n, term in enumerate(terms):
+                    nc.tensor.matmul(
+                        turned[:, t, :],
+                        term[:, t, :],
+                        identity[:],
+                        start=(n == 0),
+                        stop=(n == len(terms) - 1),
+                        is_transpose=True,
+                    )
+            first, held = rounded[0, j0 // P]
+            nc.scalar.activation(held[:, j0 - first : j0 - first + P, :], turned[:].rearrange("p t j -> p j t"), ACT.Sqrt)
 
         def quantize_envelope(g, j0, width):
             cols = slice(j0, j0 + width)
-            first = j0 // QUARTER * QUARTER if g == 0 else j0
+            first, held = rounded[g, j0 // P]
             nc.vector.quantize_mx(
                 out=h_codes[g][:, cols].bitcast(E4M3),
                 scales=h_scales[g][:, cols],
-                in_=rounded[g, first][:, j0 - first : j0 - first + width, :].rearrange("p c t -> p (c t)"),
+                in_=held[:, j0 - first : j0 - first + width, :].rearrange("p c t -> p (c t)"),
             )
 
-        def quantize_block(part, a):
+        def quantize_block(part, a, pairs):
             key = (part, PASS, a)
             w_codes[key] = keep.tile([P, PASS], U32, name="wc_%s%d_%d" % key, align_bytes=64)
             w_scales[key] = keep.tile([P, PASS], U8, name="ws_%s%d_%d" % key, align_bytes=64)
             source = raw[key].rearrange("p j (m t) -> p m j t", t=PACK)
-            pairs = []
             for u in range(2):
-                if (part, a) == ("i", 1):
-                    pair = keep.tile([P, 2, P, PACK], BF16, name="after_block%d" % u, align_bytes=64)
-                else:
-                    pair = stage.tile([P, 2, P, PACK], BF16, name="block_pair", align_bytes=64, bufs=3)
-                nc.vector.tensor_copy(pair[:].rearrange("p t m j -> p m j t"), source[:, :, :, 2 * u : 2 * u + 2])
-                pairs.append(pair)
+                nc.vector.tensor_copy(pairs[u].rearrange("p t m j -> p m j t"), source[:, :, :, 2 * u : 2 * u + 2])
             for u in range(2):
                 cols = slice(2 * u * P, (2 * u + 2) * P)
                 nc.vector.quantize_mx(
                     out=w_codes[key][:, cols].bitcast(E4M3),
                     scales=w_scales[key][:, cols],
-                    in_=pairs[u][:].rearrange("p t m j -> p (t m j)"),
+                    in_=pairs[u].rearrange("p t m j -> p (t m j)"),
                 )
 
-        squares = {}
+        def pair_buffers(names):
+            return [keep.tile([P, 2, P, PACK], BF16, name=name, align_bytes=64)[:] for name in names]
 
-        def block_pass(acc, part, a, t, cols, start, stop):
-            rows = slice(t * P, (t + 1) * P)
-            nc.tensor.matmul_mx(
-                out=acc,
-                lhsT=w_codes[part, PASS, a][:, rows].bitcast(E4M3),
-                lhsT_scale=w_scales[part, PASS, a][:, rows],
-                rhs=v_codes[a][:, cols].bitcast(E5M2),
-                rhs_scale=v_scales[a][:, cols],
-                start=start,
-                stop=stop,
-            )
+        block_squares = {}
 
-        def open_bank(part, j0, width, t0, a):
-            per_bank = PASS // width
-            acc = psum.tile([P, per_bank, width], F32, name="sums", bufs=BANKS)
-            for i in range(per_bank):
-                block_pass(acc[:, i, :], part, a, t0 + i, slice(j0, j0 + width), i == 0, False)
-            return acc
+        def block_sums(part, q, banks, spent=None):
+            name = spent or "block_squares_%s%d" % (part, q)
+            block_squares[part, q] = keep.tile([P, 2, QUARTER, 2], F32, name=name, align_bytes=64)
+            cols = slice(q * QUARTER, (q + 1) * QUARTER)
+            for u in range(2):
+                acc = in_bank(banks[u], [P, 2, QUARTER])
+                first = 0 if q == 0 else 1
+                for a in (first, 1 - first):
+                    for i in range(2):
+                        rows = slice((2 * u + i) * P, (2 * u + i + 1) * P)
+                        nc.tensor.matmul_mx(
+                            out=acc[:, i, :],
+                            lhsT=w_codes[part, PASS, a][:, rows].bitcast(E4M3),
+                            lhsT_scale=w_scales[part, PASS, a][:, rows],
+                            rhs=v_codes[a][:, cols].bitcast(E5M2),
+                            rhs_scale=v_scales[a][:, cols],
+                            start=(a == first and i == 0),
+                            stop=(a != first and i == 1),
+                        )
+                nc.scalar.activation(block_squares[part, q][:, u], acc[:].rearrange("p i c -> p c i"), ACT.Square)
 
-        def close_bank(acc, part, j0, width, t0, a):
-            per_bank = PASS // width
-            if t0 == 0:
-                held = keep.tile([P, PACK, width], F32, name="squares_%s%d" % (part, j0))
-                squares[part, j0] = held[:]
-            for i in range(per_bank):
-                block_pass(acc[:, i, :], part, a, t0 + i, slice(j0, j0 + width), False, i == per_bank - 1)
-            nc.scalar.activation(squares[part, j0][:, t0 : t0 + per_bank, :], acc[:], ACT.Square)
+        def add_block(q, banks=slice(0, 2), cols=slice(0, QUARTER)):
+            real = block_squares["r", q][:, banks, cols, :]
+            nc.vector.tensor_tensor(real, real, block_squares["i", q][:, banks, cols, :], ALU.add)
 
-        def block_sums(part, j0, width):
-            first = 0 if j0 == 0 else 1
-            for t0 in range(0, PACK, PASS // width):
-                close_bank(open_bank(part, j0, width, t0, first), part, j0, width, t0, 1 - first)
-
-        power = {}
-
-        def add_block(j0, width):
-            if j0 == 0:
-                power[j0] = keep.tile([P, width // 2, PACK, 2], F32, name="after_root")
-            else:
-                power[j0] = stage.tile([P, width // 2, PACK, 2], F32, name="power", bufs=2)
-            per_bank = PASS // width
-            q0 = j0 // QUARTER * QUARTER
-            for t0 in range(0, PACK, per_bank):
-                ts = slice(t0, t0 + per_bank)
-                nc.vector.tensor_tensor(
-                    power[j0][:, :, ts, :],
-                    squares["r", q0][:, ts, j0 - q0 : j0 - q0 + width].rearrange("p t (c i) -> p c t i", i=2),
-                    squares["i", j0][:, ts, :].rearrange("p t (c i) -> p c t i", i=2),
-                    ALU.add,
-                )
-
-        def root_block(j0, width):
-            rounded[1, j0] = keep.tile([P, width, PACK], BF16, name="rounded1_%d" % j0, align_bytes=64)
+        def root_block(q, cols=slice(0, QUARTER)):
+            if cols.start == 0:
+                hold_envelope(1, q * QUARTER, QUARTER, "rounded1_%d" % q)
             nc.scalar.activation(
-                rounded[1, j0][:].rearrange("p (c i) t -> p c i t", i=2),
-                power[j0][:].rearrange("p c t i -> p c i t"),
+                rounded[1, 2 * q][1][:, cols, :].rearrange("p c (u i) -> p c u i", i=2),
+                block_squares["r", q][:, :, cols, :].rearrange("p u c i -> p c u i"),
                 ACT.Sqrt,
             )
 
         out_rows = out.rearrange("(c p) j -> p c j", p=P)
 
-        def cells(j0, width, per_bank, shared, by_scalar=()):
+        def cell_sums(j0, width, c0, count, order, bank):
             cols = slice(j0, j0 + width)
-            order = (0, 1) if shared else (1, 0)
-            for c0 in range(0, N // P, per_bank):
-                acc = psum.tile([P, per_bank, width], F32, name="sums" if shared else "turns", bufs=BANKS)
-                for g in order:
-                    for i in range(per_bank):
-                        rows = slice((c0 + i) * P, (c0 + i + 1) * P)
-                        nc.tensor.matmul_mx(
-                            out=acc[:, i, :],
-                            lhsT=w3_codes[:, g, rows].bitcast(E4M3),
-                            lhsT_scale=w3_planes[4 * g : P, rows],
-                            rhs=h_codes[g][:, cols].bitcast(E4M3),
-                            rhs_scale=h_scales[g][:, cols],
-                            start=(g == order[0] and i == 0),
-                            stop=(g == order[1] and i == per_bank - 1),
-                        )
-                if c0 in by_scalar:
-                    held = keep.tile([P, per_bank, width], F32, name="scaled" if per_bank == 4 else "first_rounded0", align_bytes=64)
-                    result = held[:]
-                else:
-                    first = N // P * j0 + c0 * width
-                    result = landing[:, first : first + per_bank * width].rearrange("p (i c) -> p i c", i=per_bank)
-                if c0 in by_scalar:
-                    for i in range(per_bank):
-                        factor = gain[:, c0 + i : c0 + i + 1]
-                        nc.scalar.activation(result[:, i, :], acc[:, i, :], ACT.Copy, scale=factor)
-                else:
-                    spread = gain[:, c0 : c0 + per_bank].unsqueeze(2).to_broadcast([P, per_bank, width])
-                    nc.vector.tensor_tensor(result, acc[:], spread, ALU.mult)
-                nc.sync.dma_start(out=out_rows[:, c0 : c0 + per_bank, cols], in_=result)
+            acc = in_bank(bank, [P, count, width])
+            for g in order:
+                for i in range(count):
+                    rows = slice((c0 + i) * P, (c0 + i + 1) * P)
+                    nc.tensor.matmul_mx(
+                        out=acc[:, i, :],
+                        lhsT=w3_codes[:, g, rows].bitcast(E4M3),
+                        lhsT_scale=w3_planes[4 * g : P, rows],
+                        rhs=h_codes[g][:, cols].bitcast(E4M3),
+                        rhs_scale=h_scales[g][:, cols],
+                        start=(g == order[0] and i == 0),
+                        stop=(g == order[1] and i == count - 1),
+                    )
+            return acc, j0, width, c0, count
+
+        def scale_and_store(sums, own=None):
+            acc, j0, width, c0, count = sums
+            if own is None:
+                first = N // P * j0 + c0 * width
+                result = landing[:, first : first + count * width].rearrange("p (i c) -> p i c", i=count)
+                spread = gain[:, c0 : c0 + count].unsqueeze(2).to_broadcast([P, count, width])
+                nc.vector.tensor_tensor(result, acc[:], spread, ALU.mult)
+            else:
+                result = keep.tile([P, count, width], F32, name=own, align_bytes=64)[:]
+                for i in range(count):
+                    factor = gain[:, c0 + i : c0 + i + 1]
+                    nc.scalar.activation(result[:, i, :], acc[:, i, :], ACT.Copy, scale=factor)
+            nc.sync.dma_start(out=out_rows[:, c0 : c0 + count, j0 : j0 + width], in_=result)
+
+        def strip_buffer(name):
+            return keep.tile([P, STRIP * PACK], BF16, name=name, align_bytes=64)[:]
 
         gather_words(0, 0, S)
         for a in range(2):
-            grouped[a] = keep.tile([P, STRIP * PACK], BF16, name="first_rounded%d" % a, align_bytes=64)
-            round_strip("r", 0, a, grouped[a][:], True)
-        load_late()
-        quantize_strip("r", 0, (0,), grouped[0][:])
-        opened = []
-        for q in range(QUARTERS):
-            acc = psum.tile([P, 2, STRIP], F32, name="sums", bufs=BANKS)
-            for i in range(2):
-                strip_pass(acc, "r", 0, 0, q, i, i == 0, False)
-            opened.append(acc)
+            round_strip("r", 0, a, strip_buffer("first_rounded%d" % a), STRIP)
+        quantize_strip("r", 0, 0)
         gather_words(1, 0, S)
-        quantize_strip("r", 0, (1,), grouped[1][:])
+        quantize_strip("r", 0, 1)
+        round_strip("i", 0, 0, strip_buffer("second_rounded0"), STRIP)
         for q in range(QUARTERS):
-            for i in range(2):
-                strip_pass(opened[q], "r", 0, 1, q, i, False, i == 1)
-            square_strip(opened[q], "r", 0, q)
+            strip_sums("r", 0, q, q)
 
         w3_codes = keep.tile([P, 2, N], U32, name="table1", align_bytes=64)
         nc.sync.dma_start(
@@ -367,68 +315,96 @@ def tile_list_residual_envelope_map_kernel(
         with nc.allow_non_contiguous_dma(reason="one value of illum for each partition"):
             nc.sync.dma_start(out=gain[:], in_=illum.rearrange("(c p) -> p c", p=P))
 
-        for part, c0 in (("i", 0), ("r", STRIP), ("i", STRIP)):
-            prepare_strip(part, c0, (0,) if c0 == 0 else ())
-            for q in range(QUARTERS - 1 if (part, c0) == ("i", STRIP) else QUARTERS):
-                strip_sums(part, c0, q)
-        early_sums = keep.tile([P, 2, PACK, P], F32, name="after_strips", align_bytes=64)
-        vector_sums[1] = early_sums[:]
-        add_strip(1, 0, STRIP)
-        quantize_block("r", 0)
-        add_strip(1, STRIP, STRIP)
-        quantize_block("r", 1)
-        turn_and_root(0)
-        strip_sums("i", STRIP, QUARTERS - 1)
-        turn_and_root(1)
-        for q in range(QUARTERS - 1):
-            block_sums("r", q * QUARTER, QUARTER)
-        last = S - QUARTER
-        close_bank(open_bank("r", last, QUARTER, 0, 1), "r", last, QUARTER, 0, 0)
+        round_strip("i", 0, 1, strip_buffer("second_rounded1"), 0)
         for a in range(2):
-            quantize_block("i", a)
-        h_scales.insert(0, keep.tile([P, S], U8, name="after_block0", align_bytes=64))
-        late_sums = keep.tile([P, 2, PACK, P], F32, name="after_block1", align_bytes=64)
-        vector_sums[2] = late_sums[:]
-        add_strip(2, 0, PASS)
+            quantize_strip("i", 0, a)
+        for q in range(QUARTERS):
+            strip_sums("i", 0, q, q)
+        for a in range(2):
+            round_strip("r", STRIP, a, strip_buffer("third_rounded%d" % a), 0)
+        for a in range(2):
+            quantize_strip("r", STRIP, a)
+        for q in range(QUARTERS):
+            strip_sums("r", STRIP, q, q)
+        both = keep.tile([P, 2, STRIP * PACK], BF16, name="after_strips", align_bytes=64)
+        for a in range(2):
+            round_strip("i", STRIP, a, both[:, a, :], 0)
+        for a in range(2):
+            quantize_strip("i", STRIP, a)
+        for q in range(QUARTERS - 1):
+            strip_sums("i", STRIP, q, q)
 
-        for j0 in (0, QUARTER):
-            block_sums("i", j0, QUARTER)
-            add_block(j0, QUARTER)
-        for j0 in (0, QUARTER):
-            quantize_envelope(0, j0, QUARTER)
-            root_block(j0, QUARTER)
-            quantize_envelope(1, j0, QUARTER)
-        turn_and_root(2)
-        cells(0, QUARTER, 2, False)
-        quantize_envelope(0, 2 * QUARTER, QUARTER)
-
-        units = list(range(S // 2, S, P))
-
-        def sums_and_add(j0):
-            block_sums("i", j0, P)
-            add_block(j0, P)
-
-        def envelope(j0):
-            root_block(j0, P)
-            quantize_envelope(1, j0, P)
-
-        for j0 in units[:2]:
-            sums_and_add(j0)
-        cells(QUARTER, QUARTER, 2, False)
-        last_sums = keep.tile([P, 2, PACK, P], F32, name="after_root")
-        vector_sums[3] = last_sums[:]
-        add_strip(3, 0, PASS)
-        close_bank(open_bank("r", last, QUARTER, 2, 1), "r", last, QUARTER, 2, 0)
-        for j0 in units[:2]:
-            envelope(j0)
+        hold_envelope(0, 0, 2 * QUARTER, "table0")
+        early = keep.tile([P, 2, PACK, P], F32, name="after_strips", align_bytes=64)
         for i in range(2):
-            sums_and_add(units[2 + i])
-            turn_and_root(3, (i,))
-            quantize_envelope(0, units[2 + i], P)
-            if i == 0:
-                cells(units[0], P, 4, False)
-        for j0 in units[2:]:
-            envelope(j0)
-        cells(units[1], P, 4, False)
-        cells(units[2], P, 4, True, (0,))
-        cells(units[3], P, 2, True, (2,))
+            strip_power[1, i] = early[:, i]
+        half = P // 2
+        add_strip(1, slice(0, 2), slice(0, half), early[:, :, :, 0:half])
+        quantize_block("r", 0, pair_buffers(("pair0", "pair1")))
+        add_strip(1, slice(0, 2), slice(half, P), early[:, :, :, half:P])
+        quantize_block("r", 1, pair_buffers(("pair2", "pair3")))
+        for i in range(2):
+            turn_and_root(0, i, 4 + i)
+        strip_sums("i", STRIP, QUARTERS - 1, 0)
+        for i in range(2):
+            turn_and_root(1, i, 6 + i)
+        add_tile(2, 0, "pair2")
+        for q in range(QUARTERS):
+            block_sums("r", q, (3, 0) if q % 2 else (1, 2))
+        quantize_block("i", 0, pair_buffers(("pair0", "pair1")))
+        quantize_block("i", 1, pair_buffers(("after_block0", "after_block1")))
+
+        after = keep.tile([P, 2, PACK, P], F32, name="after_block1", align_bytes=64)
+        strip_power[2, 1] = after[:, 0]
+        strip_power[3, 0] = after[:, 1]
+        add_strip(2, 1, slice(0, P), strip_power[2, 1])
+        h_scales[0] = keep.tile([P, S], U8, name="after_block0", align_bytes=64)
+        quantize_envelope(0, 0, 2 * QUARTER)
+        add_strip(3, 0, slice(0, P), strip_power[3, 0])
+        halves = (slice(0, P), slice(P, QUARTER))
+        block_sums("i", 0, (1, 2))
+        for u in range(2):
+            add_block(0, slice(u, u + 1))
+        block_sums("i", 1, (3, 0))
+        for u in range(2):
+            add_block(1, slice(u, u + 1))
+        root_block(0)
+        quantize_envelope(1, 0, QUARTER)
+        add_tile(3, 1, "rounded1_0")
+        hold_envelope(0, 2 * QUARTER, QUARTER, "block_squares_r0")
+        for i in range(2):
+            turn_and_root(2, i, 4 + i)
+        first = [cell_sums(0, QUARTER, c0, 2, (0, 1), 6 + c0 // 2) for c0 in (0, 2)]
+        quantize_envelope(0, 2 * QUARTER, QUARTER)
+        root_block(1)
+        for sums in first:
+            scale_and_store(sums)
+        quantize_envelope(1, QUARTER, QUARTER)
+        block_sums("i", 2, (3, 0), "block_squares_r1")
+        for u in range(2):
+            add_block(2, slice(u, u + 1))
+        second = [cell_sums(QUARTER, QUARTER, c0, 2, (0, 1), 1 + c0 // 2) for c0 in (0, 2)]
+        block_sums("i", 3, (5, 6), "block_squares_i0")
+        scale_and_store(second[0])
+        add_block(3)
+        root_block(2)
+        quantize_envelope(1, 2 * QUARTER, QUARTER)
+        scale_and_store(second[1])
+        third = [cell_sums(2 * QUARTER, QUARTER, c0, 2, (0, 1), (6, 1)[c0 // 2]) for c0 in (0, 2)]
+        hold_envelope(0, 3 * QUARTER, P, "block_squares_r2")
+        turn_and_root(3, 0, 3)
+        quantize_envelope(0, 3 * QUARTER, P)
+        root_block(3, halves[0])
+        quantize_envelope(1, 3 * QUARTER, P)
+        scale_and_store(third[0])
+        root_block(3, halves[1])
+        quantize_envelope(1, S - P, P)
+        fourth = [cell_sums(3 * QUARTER, P, c0, 2, (0, 1), (7, 0)[c0 // 2]) for c0 in (0, 2)]
+        hold_envelope(0, S - P, P, "block_squares_r3")
+        turn_and_root(3, 1, 4)
+        quantize_envelope(0, S - P, P)
+        scale_and_store(fourth[0])
+        scale_and_store(third[1], "first_strip0")
+        scale_and_store(fourth[1], "first_rounded0")
+        scale_and_store(cell_sums(S - P, P, 0, 2, (1, 0), 5))
+        scale_and_store(cell_sums(S - P, P, 2, 2, (1, 0), 2), "second_rounded0")

@@ -246,10 +246,10 @@ def tile_list_residual_envelope_map_kernel(
             nc.vector.tensor_tensor(real, real, block_squares["i", q][:, banks, cols, :], ALU.add)
 
         def root_block(q, cols=slice(0, QUARTER)):
-            if cols.start == 0:
-                hold_envelope(1, q * QUARTER, QUARTER, "rounded1_%d" % q)
+            j0 = q * QUARTER + cols.start
+            hold_envelope(1, j0, cols.stop - cols.start, "rounded1_%d" % j0)
             nc.scalar.activation(
-                rounded[1, 2 * q][1][:, cols, :].rearrange("p c (u i) -> p c u i", i=2),
+                rounded[1, j0 // P][1][:].rearrange("p c (u i) -> p c u i", i=2),
                 block_squares["r", q][:, :, cols, :].rearrange("p u c i -> p c u i"),
                 ACT.Sqrt,
             )
@@ -273,18 +273,16 @@ def tile_list_residual_envelope_map_kernel(
                     )
             return acc, j0, width, c0, count
 
-        def scale_and_store(sums, own=None):
+        def scale_and_store(sums, spent, on_scalar=False):
             acc, j0, width, c0, count = sums
-            if own is None:
-                first = N // P * j0 + c0 * width
-                result = landing[:, first : first + count * width].rearrange("p (i c) -> p i c", i=count)
-                spread = gain[:, c0 : c0 + count].unsqueeze(2).to_broadcast([P, count, width])
-                nc.vector.tensor_tensor(result, acc[:], spread, ALU.mult)
-            else:
-                result = keep.tile([P, count, width], F32, name=own, align_bytes=64)[:]
+            result = keep.tile([P, count, width], F32, name=spent, align_bytes=64)[:]
+            if on_scalar:
                 for i in range(count):
                     factor = gain[:, c0 + i : c0 + i + 1]
                     nc.scalar.activation(result[:, i, :], acc[:, i, :], ACT.Copy, scale=factor)
+            else:
+                spread = gain[:, c0 : c0 + count].unsqueeze(2).to_broadcast([P, count, width])
+                nc.vector.tensor_tensor(result, acc[:], spread, ALU.mult)
             nc.sync.dma_start(out=out_rows[:, c0 : c0 + count, j0 : j0 + width], in_=result)
 
         def strip_buffer(name):
@@ -370,41 +368,39 @@ def tile_list_residual_envelope_map_kernel(
             add_block(1, slice(u, u + 1))
         root_block(0)
         quantize_envelope(1, 0, QUARTER)
-        add_tile(3, 1, "rounded1_0")
-        hold_envelope(0, 2 * QUARTER, QUARTER, "block_squares_r0")
-        for i in range(2):
-            turn_and_root(2, i, 4 + i)
-        first = [cell_sums(0, QUARTER, c0, 2, (0, 1), 6 + c0 // 2) for c0 in (0, 2)]
-        quantize_envelope(0, 2 * QUARTER, QUARTER)
-        root_block(1)
-        for sums in first:
-            scale_and_store(sums)
-        quantize_envelope(1, QUARTER, QUARTER)
-        block_sums("i", 2, (3, 0), "block_squares_r1")
+        add_tile(3, 1, "block_squares_i1")
+        block_sums("i", 2, (1, 2), "block_squares_r0")
         for u in range(2):
             add_block(2, slice(u, u + 1))
-        second = [cell_sums(QUARTER, QUARTER, c0, 2, (0, 1), 1 + c0 // 2) for c0 in (0, 2)]
-        block_sums("i", 3, (5, 6), "block_squares_i0")
-        scale_and_store(second[0])
-        add_block(3)
+        first = [cell_sums(0, QUARTER, c0, 2, (0, 1), 6 + c0 // 2) for c0 in (0, 2)]
+        root_block(1)
+        scale_and_store(first[0], "pair0")
+        quantize_envelope(1, QUARTER, QUARTER)
+        scale_and_store(first[1], "pair1")
+        hold_envelope(0, 2 * QUARTER, QUARTER, "block_squares_r1")
+        for i in range(2):
+            turn_and_root(2, i, 4 + i)
+        quantize_envelope(0, 2 * QUARTER, QUARTER)
+        second = [cell_sums(QUARTER, QUARTER, c0, 2, (0, 1), (3, 0)[c0 // 2]) for c0 in (0, 2)]
+        scale_and_store(second[0], "pair3")
         root_block(2)
+        scale_and_store(second[1], "third_rounded0")
         quantize_envelope(1, 2 * QUARTER, QUARTER)
-        scale_and_store(second[1])
-        third = [cell_sums(2 * QUARTER, QUARTER, c0, 2, (0, 1), (6, 1)[c0 // 2]) for c0 in (0, 2)]
-        hold_envelope(0, 3 * QUARTER, P, "block_squares_r2")
-        turn_and_root(3, 0, 3)
-        quantize_envelope(0, 3 * QUARTER, P)
-        root_block(3, halves[0])
-        quantize_envelope(1, 3 * QUARTER, P)
-        scale_and_store(third[0])
-        root_block(3, halves[1])
-        quantize_envelope(1, S - P, P)
-        fourth = [cell_sums(3 * QUARTER, P, c0, 2, (0, 1), (7, 0)[c0 // 2]) for c0 in (0, 2)]
-        hold_envelope(0, S - P, P, "block_squares_r3")
-        turn_and_root(3, 1, 4)
-        quantize_envelope(0, S - P, P)
-        scale_and_store(fourth[0])
-        scale_and_store(third[1], "first_strip0")
-        scale_and_store(fourth[1], "first_rounded0")
-        scale_and_store(cell_sums(S - P, P, 0, 2, (1, 0), 5))
-        scale_and_store(cell_sums(S - P, P, 2, 2, (1, 0), 2), "second_rounded0")
+        block_sums("i", 3, (1, 2), "block_squares_r2")
+        for u in range(2):
+            add_block(3, slice(u, u + 1))
+        third = [cell_sums(2 * QUARTER, QUARTER, c0, 2, (0, 1), 6 + c0 // 2) for c0 in (0, 2)]
+        scale_and_store(third[0], "third_rounded1")
+        hold_envelope(0, 3 * QUARTER, QUARTER, "rounded0_last")
+        for i in range(2):
+            turn_and_root(3, i, 4 + i)
+        quantize_envelope(0, 3 * QUARTER, QUARTER)
+        for i in range(2):
+            j0 = 3 * QUARTER + i * P
+            root_block(3, halves[i])
+            quantize_envelope(1, j0, P)
+        scale_and_store(third[1], "table0", True)
+        for i in range(2):
+            j0 = 3 * QUARTER + i * P
+            scale_and_store(cell_sums(j0, P, 0, 2, (0, 1), (3, 1)[i]), ("first_strip0", "second_rounded1")[i])
+            scale_and_store(cell_sums(j0, P, 2, 2, (0, 1), (0, 2)[i]), ("first_rounded0", "second_rounded0")[i], True)

@@ -39,12 +39,12 @@ def tile_list_residual_envelope_map_kernel(
         offsets = keep.tile([P, S // 16], U16, name="offsets")
         nc.sync.dma_start(offsets[:], offs)
 
-        scale_window = keep.tile([P, T], U8, name="late_loads", align_bytes=64)
+        scale_window = keep.tile([P, T], U8, name="late_loads", align_bytes=256)
         nc.vector.memset(scale_window[:].bitcast(I32), 0)
         by_row = tab_scales.rearrange("a (q r) t -> r q a t", r=4)
         for r in range(4):
             nc.sync.dma_start(out=scale_window[r:P:16, :].bitcast(I32), in_=by_row[r].bitcast(I32))
-        moved_scales = keep.tile([P, S], U8, name="moved_scales", align_bytes=64)
+        moved_scales = keep.tile([P, S], U8, name="moved_scales", align_bytes=256)
         nc.vector.memset(moved_scales[:].bitcast(I32), 0)
         warm_in = keep.tile([P, 1], F32, name="warm_in")
         warm_out = keep.tile([P, 1], F32, name="warm_out")
@@ -58,7 +58,7 @@ def tile_list_residual_envelope_map_kernel(
         table = []
 
         def load_table(a, cuts):
-            held = keep.tile([P, T], U32, name="table%d" % a, align_bytes=64)
+            held = keep.tile([P, T], U32, name="table%d" % a, align_bytes=256)
             words = tab_words[a].rearrange("p t i -> p (t i)").bitcast(I32)
             for c0, c1 in zip(cuts[:-1], cuts[1:]):
                 nc.sync.dma_start(out=held[:].bitcast(I32)[:, c0:c1], in_=words[:, c0:c1])
@@ -74,23 +74,23 @@ def tile_list_residual_envelope_map_kernel(
         for a in range(2):
             if a == 1:
                 load_table(1, (0, T))
-            first = keep.tile([P, PACK * STRIP], F32, name="first_strip%d" % a, align_bytes=64)
+            first = keep.tile([P, PACK * STRIP], F32, name="first_strip%d" % a, align_bytes=256)
             load_weights(first[:], "r", 0, STRIP, a)
 
-        picked_scales = keep.tile([P, S], U8, name="picked_scales", align_bytes=64)
+        picked_scales = keep.tile([P, S], U8, name="picked_scales", align_bytes=256)
         nc.vector.tensor_copy(picked_scales[:], scale_window[:].indirect(offsets[:]))
         nc.sync.dma_start(out=moved_scales[0:112, :].bitcast(I32), in_=picked_scales[16:P, :].bitcast(I32))
         v_scales = [picked_scales, moved_scales]
 
         late = [("i", 0, STRIP), ("r", STRIP, STRIP), ("i", STRIP, STRIP), ("r", PASS, PASS), ("i", PASS, PASS)]
-        landing = keep.tile([P, sum(2 * PACK * piece[2] for piece in late)], F32, name="late_loads", align_bytes=64)
+        landing = keep.tile([P, sum(2 * PACK * piece[2] for piece in late)], F32, name="late_loads", align_bytes=256)
         at = 0
         for part, c0, width in late:
             for a in range(2):
                 load_weights(landing[:, at : at + PACK * width], part, c0, width, a)
                 at = at + PACK * width
 
-        v_codes = [keep.tile([P, S], U32, name="v_codes%d" % a, align_bytes=64) for a in range(2)]
+        v_codes = [keep.tile([P, S], U32, name="v_codes%d" % a, align_bytes=256) for a in range(2)]
 
         def gather_words(a, j0, count):
             picks = offsets[:, j0 // 16 : (j0 + count) // 16]
@@ -112,8 +112,8 @@ def tile_list_residual_envelope_map_kernel(
 
         def quantize_strip(part, c0, a):
             key = (part, c0, a)
-            codes = keep.tile([P, STRIP], U32, name="wc_%s%d_%d" % key, align_bytes=64)
-            planes = keep.tile([P, STRIP], U8, name="ws_%s%d_%d" % key, align_bytes=64)
+            codes = keep.tile([P, STRIP], U32, name="wc_%s%d_%d" % key, align_bytes=256)
+            planes = keep.tile([P, STRIP], U8, name="ws_%s%d_%d" % key, align_bytes=256)
             nc.vector.quantize_mx(out=codes[:].bitcast(E4M3), scales=planes[:], in_=grouped[key])
             w_codes[key] = codes[:]
             w_scales[key] = planes[:]
@@ -158,27 +158,25 @@ def tile_list_residual_envelope_map_kernel(
             )
 
         def add_tile(q, i, spent):
-            strip_power[q, i] = keep.tile([P, PACK, P], F32, name=spent, align_bytes=64)[:]
+            strip_power[q, i] = keep.tile([P, PACK, P], F32, name=spent, align_bytes=256)[:]
             add_strip(q, i, slice(0, P), strip_power[q, i])
 
         rounded = {}
 
         def hold_envelope(g, j0, width, name):
-            held = keep.tile([P, width, PACK], BF16, name=name, align_bytes=64)
+            held = keep.tile([P, width, PACK], BF16, name=name, align_bytes=256)
             for tile in range(j0 // P, (j0 + width) // P):
                 rounded[g, tile] = (j0, held)
 
-        h_codes = [keep.tile([P, S], U32, name="h_codes%d" % g, align_bytes=64) for g in range(2)]
-        h_scales = {1: keep.tile([P, S], U8, name="h_scales1", align_bytes=64)}
+        h_codes = [keep.tile([P, S], U32, name="h_codes%d" % g, align_bytes=256) for g in range(2)]
+        h_scales = {1: keep.tile([P, S], U8, name="h_scales1", align_bytes=256)}
 
-        def turn_and_root(q, i, bank):
-            j0 = q * QUARTER + i * P
+        def turn(turned, q, i, slots):
             if (q, i) in strip_power:
                 terms = [strip_power[q, i]]
             else:
                 terms = [strip_squares["i", q][:, i], strip_squares["r", q][:, i]]
-            turned = in_bank(bank, [P, PACK, P])
-            for t in range(PACK):
+            for t in slots:
                 for n, term in enumerate(terms):
                     nc.tensor.matmul(
                         turned[:, t, :],
@@ -188,8 +186,16 @@ def tile_list_residual_envelope_map_kernel(
                         stop=(n == len(terms) - 1),
                         is_transpose=True,
                     )
+
+        def root_turned(turned, q, i):
+            j0 = q * QUARTER + i * P
             first, held = rounded[0, j0 // P]
             nc.scalar.activation(held[:, j0 - first : j0 - first + P, :], turned[:].rearrange("p t j -> p j t"), ACT.Sqrt)
+
+        def turn_and_root(q, i, bank):
+            turned = in_bank(bank, [P, PACK, P])
+            turn(turned, q, i, range(PACK))
+            root_turned(turned, q, i)
 
         def quantize_envelope(g, j0, width):
             cols = slice(j0, j0 + width)
@@ -202,8 +208,8 @@ def tile_list_residual_envelope_map_kernel(
 
         def quantize_block(part, a, pairs):
             key = (part, PASS, a)
-            w_codes[key] = keep.tile([P, PASS], U32, name="wc_%s%d_%d" % key, align_bytes=64)
-            w_scales[key] = keep.tile([P, PASS], U8, name="ws_%s%d_%d" % key, align_bytes=64)
+            w_codes[key] = keep.tile([P, PASS], U32, name="wc_%s%d_%d" % key, align_bytes=256)
+            w_scales[key] = keep.tile([P, PASS], U8, name="ws_%s%d_%d" % key, align_bytes=256)
             source = raw[key].rearrange("p j (m t) -> p m j t", t=PACK)
             for u in range(2):
                 nc.vector.tensor_copy(pairs[u].rearrange("p t m j -> p m j t"), source[:, :, :, 2 * u : 2 * u + 2])
@@ -216,29 +222,42 @@ def tile_list_residual_envelope_map_kernel(
                 )
 
         def pair_buffers(names):
-            return [keep.tile([P, 2, P, PACK], BF16, name=name, align_bytes=64)[:] for name in names]
+            return [keep.tile([P, 2, P, PACK], BF16, name=name, align_bytes=256)[:] for name in names]
 
         block_squares = {}
 
-        def block_sums(part, q, banks, spent=None):
-            name = spent or "block_squares_%s%d" % (part, q)
-            block_squares[part, q] = keep.tile([P, 2, QUARTER, 2], F32, name=name, align_bytes=64)
+        def block_pass(acc, part, q, u, a, start):
             cols = slice(q * QUARTER, (q + 1) * QUARTER)
+            for i in range(2):
+                rows = slice((2 * u + i) * P, (2 * u + i + 1) * P)
+                nc.tensor.matmul_mx(
+                    out=acc[:, i, :],
+                    lhsT=w_codes[part, PASS, a][:, rows].bitcast(E4M3),
+                    lhsT_scale=w_scales[part, PASS, a][:, rows],
+                    rhs=v_codes[a][:, cols].bitcast(E5M2),
+                    rhs_scale=v_scales[a][:, cols],
+                    start=(start and i == 0),
+                    stop=(not start and i == 1),
+                )
+
+        def open_block(part, q, banks):
+            opened = [in_bank(bank, [P, 2, QUARTER]) for bank in banks]
             for u in range(2):
-                acc = in_bank(banks[u], [P, 2, QUARTER])
-                first = 0 if q == 0 else 1
-                for a in (first, 1 - first):
-                    for i in range(2):
-                        rows = slice((2 * u + i) * P, (2 * u + i + 1) * P)
-                        nc.tensor.matmul_mx(
-                            out=acc[:, i, :],
-                            lhsT=w_codes[part, PASS, a][:, rows].bitcast(E4M3),
-                            lhsT_scale=w_scales[part, PASS, a][:, rows],
-                            rhs=v_codes[a][:, cols].bitcast(E5M2),
-                            rhs_scale=v_scales[a][:, cols],
-                            start=(a == first and i == 0),
-                            stop=(a != first and i == 1),
-                        )
+                block_pass(opened[u], part, q, u, 0, True)
+            return opened
+
+        def block_sums(part, q, banks, spent=None, opened=None):
+            name = spent or "block_squares_%s%d" % (part, q)
+            block_squares[part, q] = keep.tile([P, 2, QUARTER, 2], F32, name=name, align_bytes=256)
+            for u in range(2):
+                if opened is None:
+                    acc = in_bank(banks[u], [P, 2, QUARTER])
+                    first = 0 if q == 0 else 1
+                    block_pass(acc, part, q, u, first, True)
+                    block_pass(acc, part, q, u, 1 - first, False)
+                else:
+                    acc = opened[u]
+                    block_pass(acc, part, q, u, 1, False)
                 nc.scalar.activation(block_squares[part, q][:, u], acc[:].rearrange("p i c -> p c i"), ACT.Square)
 
         def add_block(q, banks=slice(0, 2), cols=slice(0, QUARTER)):
@@ -275,7 +294,7 @@ def tile_list_residual_envelope_map_kernel(
 
         def scale_and_store(sums, spent, on_scalar=False):
             acc, j0, width, c0, count = sums
-            result = keep.tile([P, count, width], F32, name=spent, align_bytes=64)[:]
+            result = keep.tile([P, count, width], F32, name=spent, align_bytes=256)[:]
             if on_scalar:
                 for i in range(count):
                     factor = gain[:, c0 + i : c0 + i + 1]
@@ -286,7 +305,7 @@ def tile_list_residual_envelope_map_kernel(
             nc.sync.dma_start(out=out_rows[:, c0 : c0 + count, j0 : j0 + width], in_=result)
 
         def strip_buffer(name):
-            return keep.tile([P, STRIP * PACK], BF16, name=name, align_bytes=64)[:]
+            return keep.tile([P, STRIP * PACK], BF16, name=name, align_bytes=256)[:]
 
         gather_words(0, 0, S)
         for a in range(2):
@@ -298,18 +317,18 @@ def tile_list_residual_envelope_map_kernel(
         for q in range(QUARTERS):
             strip_sums("r", 0, q, q)
 
-        w3_codes = keep.tile([P, 2, N], U32, name="table1", align_bytes=64)
+        w3_codes = keep.tile([P, 2, N], U32, name="table1", align_bytes=256)
         nc.sync.dma_start(
             out=w3_codes[:].bitcast(I32), in_=w3_words.rearrange("a p c i -> p a (c i)").bitcast(I32)
         )
-        w3_planes = keep.tile([P, N], U8, name="first_rounded1", align_bytes=64)
+        w3_planes = keep.tile([P, N], U8, name="first_rounded1", align_bytes=256)
         nc.gpsimd.memset(w3_planes[:].bitcast(I32), 0)
         for q in range(4):
             nc.sync.dma_start(
                 out=w3_planes[32 * q : 32 * q + 8, :].bitcast(I32),
                 in_=w3_scales[:, 4 * q : 4 * q + 4, :].bitcast(I32),
             )
-        gain = keep.tile([P, N // P], F32, name="first_strip1", align_bytes=64)
+        gain = keep.tile([P, N // P], F32, name="first_strip1", align_bytes=256)
         with nc.allow_non_contiguous_dma(reason="one value of illum for each partition"):
             nc.sync.dma_start(out=gain[:], in_=illum.rearrange("(c p) -> p c", p=P))
 
@@ -324,16 +343,16 @@ def tile_list_residual_envelope_map_kernel(
             quantize_strip("r", STRIP, a)
         for q in range(QUARTERS):
             strip_sums("r", STRIP, q, q)
-        both = keep.tile([P, 2, STRIP * PACK], BF16, name="after_strips", align_bytes=64)
+        both = keep.tile([P, 2, STRIP * PACK], BF16, name="after_strips", align_bytes=256)
         for a in range(2):
             round_strip("i", STRIP, a, both[:, a, :], 0)
         for a in range(2):
             quantize_strip("i", STRIP, a)
-        for q in range(QUARTERS - 1):
-            strip_sums("i", STRIP, q, q)
+        for q, bank in enumerate((0, 1, 3)):
+            strip_sums("i", STRIP, q, bank)
 
         hold_envelope(0, 0, 2 * QUARTER, "table0")
-        early = keep.tile([P, 2, PACK, P], F32, name="after_strips", align_bytes=64)
+        early = keep.tile([P, 2, PACK, P], F32, name="after_strips", align_bytes=256)
         for i in range(2):
             strip_power[1, i] = early[:, i]
         half = P // 2
@@ -341,9 +360,12 @@ def tile_list_residual_envelope_map_kernel(
         quantize_block("r", 0, pair_buffers(("pair0", "pair1")))
         add_strip(1, slice(0, 2), slice(half, P), early[:, :, :, half:P])
         quantize_block("r", 1, pair_buffers(("pair2", "pair3")))
-        for i in range(2):
-            turn_and_root(0, i, 4 + i)
+        turn_and_root(0, 0, 4)
+        parted = in_bank(5, [P, PACK, P])
+        turn(parted, 0, 1, range(PACK // 2))
         strip_sums("i", STRIP, QUARTERS - 1, 0)
+        turn(parted, 0, 1, range(PACK // 2, PACK))
+        root_turned(parted, 0, 1)
         for i in range(2):
             turn_and_root(1, i, 6 + i)
         add_tile(2, 0, "pair2")
@@ -352,11 +374,11 @@ def tile_list_residual_envelope_map_kernel(
         quantize_block("i", 0, pair_buffers(("pair0", "pair1")))
         quantize_block("i", 1, pair_buffers(("after_block0", "after_block1")))
 
-        after = keep.tile([P, 2, PACK, P], F32, name="after_block1", align_bytes=64)
+        after = keep.tile([P, 2, PACK, P], F32, name="after_block1", align_bytes=256)
         strip_power[2, 1] = after[:, 0]
         strip_power[3, 0] = after[:, 1]
         add_strip(2, 1, slice(0, P), strip_power[2, 1])
-        h_scales[0] = keep.tile([P, S], U8, name="after_block0", align_bytes=64)
+        h_scales[0] = keep.tile([P, S], U8, name="after_block0", align_bytes=256)
         quantize_envelope(0, 0, 2 * QUARTER)
         add_strip(3, 0, slice(0, P), strip_power[3, 0])
         halves = (slice(0, P), slice(P, QUARTER))
@@ -390,11 +412,12 @@ def tile_list_residual_envelope_map_kernel(
         for u in range(2):
             add_block(3, slice(u, u + 1))
         third = [cell_sums(2 * QUARTER, QUARTER, c0, 2, (0, 1), 6 + c0 // 2) for c0 in (0, 2)]
-        scale_and_store(third[0], "third_rounded1")
-        hold_envelope(0, 3 * QUARTER, QUARTER, "rounded0_last")
         for i in range(2):
+            hold_envelope(0, 3 * QUARTER + i * P, P, "rounded0_unit%d" % i)
             turn_and_root(3, i, 4 + i)
-        quantize_envelope(0, 3 * QUARTER, QUARTER)
+            quantize_envelope(0, 3 * QUARTER + i * P, P)
+            if i == 0:
+                scale_and_store(third[0], "rounded0_unit0")
         for i in range(2):
             j0 = 3 * QUARTER + i * P
             root_block(3, halves[i])

@@ -317,6 +317,18 @@ def tile_list_residual_envelope_map_kernel(
         for q in range(QUARTERS):
             strip_sums("r", 0, q, q)
 
+        unread = in_bank(7, [P, PASS])
+        for half in range(2):
+            nc.tensor.matmul_mx(
+                out=unread[:],
+                lhsT=w_codes["r", 0, 0][:, 0:P].bitcast(E4M3),
+                lhsT_scale=w_scales["r", 0, 0][:, 0:P],
+                rhs=v_codes[0][:, half * PASS : (half + 1) * PASS].bitcast(E5M2),
+                rhs_scale=v_scales[0][:, half * PASS : (half + 1) * PASS],
+                start=True,
+                stop=True,
+            )
+
         w3_codes = keep.tile([P, 2, N], U32, name="table1", align_bytes=256)
         nc.sync.dma_start(
             out=w3_codes[:].bitcast(I32), in_=w3_words.rearrange("a p c i -> p a (c i)").bitcast(I32)
@@ -416,6 +428,17 @@ def tile_list_residual_envelope_map_kernel(
             hold_envelope(0, 3 * QUARTER + i * P, P, "rounded0_unit%d" % i)
             turn_and_root(3, i, 4 + i)
             quantize_envelope(0, 3 * QUARTER + i * P, P)
+            unread = in_bank(4 + i, [P, PASS])
+            cols = slice(3 * QUARTER + (i + 1) * P - PASS, 3 * QUARTER + (i + 1) * P)
+            nc.tensor.matmul_mx(
+                out=unread[:],
+                lhsT=w3_codes[:, 0, 0:P].bitcast(E4M3),
+                lhsT_scale=w3_planes[:, 0:P],
+                rhs=h_codes[0][:, cols].bitcast(E4M3),
+                rhs_scale=h_scales[0][:, cols],
+                start=True,
+                stop=True,
+            )
             if i == 0:
                 scale_and_store(third[0], "rounded0_unit0")
         for i in range(2):

@@ -439,13 +439,11 @@ def tile_list_residual_envelope_map_kernel(
                 start=True,
                 stop=True,
             )
-            if i == 0:
-                scale_and_store(third[0], "rounded0_unit0")
+            scale_and_store(third[i], "rounded0_unit%d" % i)
         for i in range(2):
             j0 = 3 * QUARTER + i * P
             root_block(3, halves[i])
             quantize_envelope(1, j0, P)
-        scale_and_store(third[1], "table0", True)
         for i in range(2):
             j0 = 3 * QUARTER + i * P
             scale_and_store(cell_sums(j0, P, 0, 2, (0, 1), (3, 1)[i]), ("first_strip0", "second_rounded1")[i])

from contextlib import ExitStack

import concourse.mybir as mybir
from concourse.masks import make_identity

K, T, S, H, N = 1024, 2048, 1024, 1024, 512
FLOPS = 2 * (2 * K * H * S + H * N * S)

F32 = mybir.dt.float32
BF16 = mybir.dt.bfloat16
I32 = mybir.dt.int32
U32 = mybir.dt.uint32
U16 = mybir.dt.uint16
U8 = mybir.dt.uint8
E4M3 = mybir.dt.float8_e4m3fn_x4
E5M2 = mybir.dt.float8_e5m2_x4
ACT = mybir.ActivationFunctionType
ALU = mybir.AluOpType

P = 128
PACK = 4
PASS = P * PACK
QUARTER = 256
QUARTERS = S // QUARTER
STRIP = 256


def tile_list_residual_envelope_map_kernel(
    tc, tab_words, tab_scales, offs, wr, wi, w3_words, w3_scales, illum, out
):
    nc = tc.nc
    with ExitStack() as ctx:
        keep = ctx.enter_context(tc.tile_pool(name="keep", bufs=1))
        psum = ctx.enter_context(tc.psum_pool(name="psum", bufs=1))

        def in_bank(bank, shape):
            return psum.tile(shape, F32, name="bank%d" % bank)

        offsets = keep.tile([P, S // 16], U16, name="offsets")
        nc.sync.dma_start(offsets[:], offs)

        scale_window = keep.tile([P, T], U8, name="late_loads", align_bytes=256)
        nc.vector.memset(scale_window[:].bitcast(I32), 0)
        by_row = tab_scales.rearrange("a (q r) t -> r q a t", r=4)
        for r in range(4):
            nc.sync.dma_start(out=scale_window[r:P:16, :].bitcast(I32), in_=by_row[r].bitcast(I32))
        moved_scales = keep.tile([P, S], U8, name="moved_scales", align_bytes=256)
        nc.vector.memset(moved_scales[:].bitcast(I32), 0)
        warm_in = keep.tile([P, 1], F32, name="warm_in")
        warm_out = keep.tile([P, 1], F32, name="warm_out")
        nc.vector.memset(warm_in[:], 1.0)
        nc.scalar.activation(warm_out[:], warm_in[:], ACT.Sqrt)
        identity = keep.tile([P, P], F32, name="identity")
        make_identity(nc, identity[:])

        weights = {"r": wr, "i": wi}
        raw = {}
        table = []

        def load_table(a, cuts):
            held = keep.tile([P, T], U32, name="table%d" % a, align_bytes=256)
            words = tab_words[a].rearrange("p t i -> p (t i)").bitcast(I32)
            for c0, c1 in zip(cuts[:-1], cuts[1:]):
                nc.sync.dma_start(out=held[:].bitcast(I32)[:, c0:c1], in_=words[:, c0:c1])
            table.append(held)

        def load_weights(held, part, c0, width, a):
            rows = weights[part][a * PASS : (a + 1) * PASS, c0 : c0 + width]
            view = held.rearrange("p (j c) -> p j c", j=PACK)
            nc.sync.dma_start(out=view, in_=rows.rearrange("(p j) c -> p j c", j=PACK))
            raw[part, c0, a] = view

        load_table(0, (0, 256, 512, T))
        for a in range(2):
            if a == 1:
                load_table(1, (0, T))
            first = keep.tile([P, PACK * STRIP], F32, name="first_strip%d" % a, align_bytes=256)
            load_weights(first[:], "r", 0, STRIP, a)

        picked_scales = keep.tile([P, S], U8, name="picked_scales", align_bytes=256)
        nc.vector.tensor_copy(picked_scales[:], scale_window[:].indirect(offsets[:]))
        nc.sync.dma_start(out=moved_scales[0:112, :].bitcast(I32), in_=picked_scales[16:P, :].bitcast(I32))
        v_scales = [picked_scales, moved_scales]

        late = [("i", 0, STRIP), ("r", STRIP, STRIP), ("i", STRIP, STRIP), ("r", PASS, PASS), ("i", PASS, PASS)]
        landing = keep.tile([P, sum(2 * PACK * piece[2] for piece in late)], F32, name="late_loads", align_bytes=256)
        at = 0
        for part, c0, width in late:
            for a in range(2):
                load_weights(landing[:, at : at + PACK * width], part, c0, width, a)
                at = at + PACK * width

        v_codes = [keep.tile([P, S], U32, name="v_codes%d" % a, align_bytes=256) for a in range(2)]

        def gather_words(a, j0, count):
            picks = offsets[:, j0 // 16 : (j0 + count) // 16]
            nc.vector.tensor_copy(v_codes[a][:, j0 : j0 + count], table[a][:].indirect(picks))

        w_codes = {}
        w_scales = {}
        grouped = {}

        def round_strip(part, c0, a, target, scalar_columns):
            grouped[part, c0, a] = target
            target = target.rearrange("p (c i j) -> p c j i", i=4, j=PACK)
            source = raw[part, c0, a].rearrange("p j (c i) -> p c j i", i=4)
            cut = scalar_columns // 4
            if scalar_columns > 0:
                nc.scalar.copy(target[:, :cut], source[:, :cut])
            if scalar_columns < STRIP:
                nc.vector.tensor_copy(target[:, cut:], source[:, cut:])

        def quantize_strip(part, c0, a):
            key = (part, c0, a)
            codes = keep.tile([P, STRIP], U32, name="wc_%s%d_%d" % key, align_bytes=256)
            planes = keep.tile([P, STRIP], U8, name="ws_%s%d_%d" % key, align_bytes=256)
            nc.vector.quantize_mx(out=codes[:].bitcast(E4M3), scales=planes[:], in_=grouped[key])
            w_codes[key] = codes[:]
            w_scales[key] = planes[:]

        def strip_pass(acc, part, c0, a, q, first):
            for i in range(2):
                cols = slice(q * QUARTER + i * P, q * QUARTER + (i + 1) * P)
                nc.tensor.matmul_mx(
                    out=acc[:, i, :],
                    lhsT=v_codes[a][:, cols].bitcast(E5M2),
                    lhsT_scale=v_scales[a][:, cols],
                    rhs=w_codes[part, c0, a].bitcast(E4M3),
                    rhs_scale=w_scales[part, c0, a],
                    start=(a == first and i == 0),
                    stop=(a != first and i == 1),
                )

        strip_squares = {}

        def square_strip(acc, part, c0, q):
            if (part, q) not in strip_squares:
                strip_squares[part, q] = keep.tile([P, 2, PACK, P], F32, name="strip_squares_%s%d" % (part, q))
            m0 = c0 // PACK
            nc.scalar.activation(
                strip_squares[part, q][:, :, :, m0 : m0 + STRIP // PACK],
                acc[:].rearrange("p i (m t) -> p i t m", t=PACK),
                ACT.Square,
            )

        def strip_sums(part, c0, q, bank):
            acc = in_bank(bank, [P, 2, STRIP])
            first = 0 if q == 0 or (part, c0) == ("r", 0) else 1
            for a in (first, 1 - first):
                strip_pass(acc, part, c0, a, q, first)
            square_strip(acc, part, c0, q)

        strip_power = {}

        def add_strip(q, i, ms, target):
            nc.vector.tensor_tensor(
                target, strip_squares["r", q][:, i, :, ms], strip_squares["i", q][:, i, :, ms], ALU.add
            )

        def add_tile(q, i, spent):
            strip_power[q, i] = keep.tile([P, PACK, P], F32, name=spent, align_bytes=256)[:]
            add_strip(q, i, slice(0, P), strip_power[q, i])

        rounded = {}

        def hold_envelope(g, j0, width, name):
            held = keep.tile([P, width, PACK], BF16, name=name, align_bytes=256)
            for tile in range(j0 // P, (j0 + width) // P):
                rounded[g, tile] = (j0, held)

        h_codes = [keep.tile([P, S], U32, name="h_codes%d" % g, align_bytes=256) for g in range(2)]
        h_scales = {1: keep.tile([P, S], U8, name="h_scales1", align_bytes=256)}

        def turn(turned, q, i, slots):
            if (q, i) in strip_power:
                terms = [strip_power[q, i]]
            else:
                terms = [strip_squares["i", q][:, i], strip_squares["r", q][:, i]]
            for t in slots:
                for n, term in enumerate(terms):
                    nc.tensor.matmul(
                        turned[:, t, :],
                        term[:, t, :],
                        identity[:],
                        start=(n == 0),
                        stop=(n == len(terms) - 1),
                        is_transpose=True,
                    )

        def root_turned(turned, q, i):
            j0 = q * QUARTER + i * P
            first, held = rounded[0, j0 // P]
            nc.scalar.activation(held[:, j0 - first : j0 - first + P, :], turned[:].rearrange("p t j -> p j t"), ACT.Sqrt)

        def turn_and_root(q, i, bank):
            turned = in_bank(bank, [P, PACK, P])
            turn(turned, q, i, range(PACK))
            root_turned(turned, q, i)

        def quantize_envelope(g, j0, width):
            cols = slice(j0, j0 + width)
            first, held = rounded[g, j0 // P]
            nc.vector.quantize_mx(
                out=h_codes[g][:, cols].bitcast(E4M3),
                scales=h_scales[g][:, cols],
                in_=held[:, j0 - first : j0 - first + width, :].rearrange("p c t -> p (c t)"),
            )

        def quantize_block(part, a, pairs):
            key = (part, PASS, a)
            w_codes[key] = keep.tile([P, PASS], U32, name="wc_%s%d_%d" % key, align_bytes=256)
            w_scales[key] = keep.tile([P, PASS], U8, name="ws_%s%d_%d" % key, align_bytes=256)
            source = raw[key].rearrange("p j (m t) -> p m j t", t=PACK)
            for u in range(2):
                nc.vector.tensor_copy(pairs[u].rearrange("p t m j -> p m j t"), source[:, :, :, 2 * u : 2 * u + 2])
            for u in range(2):
                cols = slice(2 * u * P, (2 * u + 2) * P)
                nc.vector.quantize_mx(
                    out=w_codes[key][:, cols].bitcast(E4M3),
                    scales=w_scales[key][:, cols],
                    in_=pairs[u].rearrange("p t m j -> p (t m j)"),
                )

        def pair_buffers(names):
            return [keep.tile([P, 2, P, PACK], BF16, name=name, align_bytes=256)[:] for name in names]

        block_squares = {}

        def block_pass(acc, part, q, u, a, start):
            cols = slice(q * QUARTER, (q + 1) * QUARTER)
            for i in range(2):
                rows = slice((2 * u + i) * P, (2 * u + i + 1) * P)
                nc.tensor.matmul_mx(
                    out=acc[:, i, :],
                    lhsT=w_codes[part, PASS, a][:, rows].bitcast(E4M3),
                    lhsT_scale=w_scales[part, PASS, a][:, rows],
                    rhs=v_codes[a][:, cols].bitcast(E5M2),
                    rhs_scale=v_scales[a][:, cols],
                    start=(start and i == 0),
                    stop=(not start and i == 1),
                )

        def open_block(part, q, banks):
            opened = [in_bank(bank, [P, 2, QUARTER]) for bank in banks]
            for u in range(2):
                block_pass(opened[u], part, q, u, 0, True)
            return opened

        def block_sums(part, q, banks, spent=None, opened=None):
            name = spent or "block_squares_%s%d" % (part, q)
            block_squares[part, q] = keep.tile([P, 2, QUARTER, 2], F32, name=name, align_bytes=256)
            for u in range(2):
                if opened is None:
                    acc = in_bank(banks[u], [P, 2, QUARTER])
                    first = 0 if q == 0 else 1
                    block_pass(acc, part, q, u, first, True)
                    block_pass(acc, part, q, u, 1 - first, False)
                else:
                    acc = opened[u]
                    block_pass(acc, part, q, u, 1, False)
                nc.scalar.activation(block_squares[part, q][:, u], acc[:].rearrange("p i c -> p c i"), ACT.Square)

        def add_block(q, banks=slice(0, 2), cols=slice(0, QUARTER)):
            real = block_squares["r", q][:, banks, cols, :]
            nc.vector.tensor_tensor(real, real, block_squares["i", q][:, banks, cols, :], ALU.add)

        def root_block(q, cols=slice(0, QUARTER)):
            j0 = q * QUARTER + cols.start
            hold_envelope(1, j0, cols.stop - cols.start, "rounded1_%d" % j0)
            nc.scalar.activation(
                rounded[1, j0 // P][1][:].rearrange("p c (u i) -> p c u i", i=2),
                block_squares["r", q][:, :, cols, :].rearrange("p u c i -> p c u i"),
                ACT.Sqrt,
            )

        out_rows = out.rearrange("(c p) j -> p c j", p=P)

        def cell_sums(j0, width, c0, count, order, bank):
            cols = slice(j0, j0 + width)
            acc = in_bank(bank, [P, count, width])
            for g in order:
                for i in range(count):
                    rows = slice((c0 + i) * P, (c0 + i + 1) * P)
                    nc.tensor.matmul_mx(
                        out=acc[:, i, :],
                        lhsT=w3_codes[:, g, rows].bitcast(E4M3),
                        lhsT_scale=w3_planes[4 * g : P, rows],
                        rhs=h_codes[g][:, cols].bitcast(E4M3),
                        rhs_scale=h_scales[g][:, cols],
                        start=(g == order[0] and i == 0),
                        stop=(g == order[1] and i == count - 1),
                    )
            return acc, j0, width, c0, count

        def scale_and_store(sums, spent, on_scalar=False):
            acc, j0, width, c0, count = sums
            result = keep.tile([P, count, width], F32, name=spent, align_bytes=256)[:]
            if on_scalar:
                for i in range(count):
                    factor = gain[:, c0 + i : c0 + i + 1]
                    nc.scalar.activation(result[:, i, :], acc[:, i, :], ACT.Copy, scale=factor)
            else:
                spread = gain[:, c0 : c0 + count].unsqueeze(2).to_broadcast([P, count, width])
                nc.vector.tensor_tensor(result, acc[:], spread, ALU.mult)
            nc.sync.dma_start(out=out_rows[:, c0 : c0 + count, j0 : j0 + width], in_=result)

        def strip_buffer(name):
            return keep.tile([P, STRIP * PACK], BF16, name=name, align_bytes=256)[:]

        gather_words(0, 0, S)
        for a in range(2):
            round_strip("r", 0, a, strip_buffer("first_rounded%d" % a), STRIP)
        quantize_strip("r", 0, 0)
        gather_words(1, 0, S)
        quantize_strip("r", 0, 1)
        round_strip("i", 0, 0, strip_buffer("second_rounded0"), STRIP)
        for q in range(QUARTERS):
            strip_sums("r", 0, q, q)

        unread = in_bank(7, [P, PASS])
        for half in range(2):
            nc.tensor.matmul_mx(
                out=unread[:],
                lhsT=w_codes["r", 0, 0][:, 0:P].bitcast(E4M3),
                lhsT_scale=w_scales["r", 0, 0][:, 0:P],
                rhs=v_codes[0][:, half * PASS : (half + 1) * PASS].bitcast(E5M2),
                rhs_scale=v_scales[0][:, half * PASS : (half + 1) * PASS],
                start=True,
                stop=True,
            )

        w3_codes = keep.tile([P, 2, N], U32, name="table1", align_bytes=256)
        nc.sync.dma_start(
            out=w3_codes[:].bitcast(I32), in_=w3_words.rearrange("a p c i -> p a (c i)").bitcast(I32)
        )
        w3_planes = keep.tile([P, N], U8, name="first_rounded1", align_bytes=256)
        nc.gpsimd.memset(w3_planes[:].bitcast(I32), 0)
        for q in range(4):
            nc.sync.dma_start(
                out=w3_planes[32 * q : 32 * q + 8, :].bitcast(I32),
                in_=w3_scales[:, 4 * q : 4 * q + 4, :].bitcast(I32),
            )
        gain = keep.tile([P, N // P], F32, name="first_strip1", align_bytes=256)
        with nc.allow_non_contiguous_dma(reason="one value of illum for each partition"):
            nc.sync.dma_start(out=gain[:], in_=illum.rearrange("(c p) -> p c", p=P))

        round_strip("i", 0, 1, strip_buffer("second_rounded1"), 0)
        for a in range(2):
            quantize_strip("i", 0, a)
        for q in range(QUARTERS):
            strip_sums("i", 0, q, q)
        for a in range(2):
            round_strip("r", STRIP, a, strip_buffer("third_rounded%d" % a), 0)
        for a in range(2):
            quantize_strip("r", STRIP, a)
        for q in range(QUARTERS):
            strip_sums("r", STRIP, q, q)
        both = keep.tile([P, 2, STRIP * PACK], BF16, name="after_strips", align_bytes=256)
        for a in range(2):
            round_strip("i", STRIP, a, both[:, a, :], 0)
        for a in range(2):
            quantize_strip("i", STRIP, a)
        for q, bank in enumerate((0, 1, 3)):
            strip_sums("i", STRIP, q, bank)

        hold_envelope(0, 0, 2 * QUARTER, "table0")
        early = keep.tile([P, 2, PACK, P], F32, name="after_strips", align_bytes=256)
        for i in range(2):
            strip_power[1, i] = early[:, i]
        half = P // 2
        add_strip(1, slice(0, 2), slice(0, half), early[:, :, :, 0:half])
        quantize_block("r", 0, pair_buffers(("pair0", "pair1")))
        add_strip(1, slice(0, 2), slice(half, P), early[:, :, :, half:P])
        quantize_block("r", 1, pair_buffers(("pair2", "pair3")))
        turn_and_root(0, 0, 4)
        parted = in_bank(5, [P, PACK, P])
        turn(parted, 0, 1, range(PACK // 2))
        strip_sums("i", STRIP, QUARTERS - 1, 0)
        turn(parted, 0, 1, range(PACK // 2, PACK))
        root_turned(parted, 0, 1)
        for i in range(2):
            turn_and_root(1, i, 6 + i)
        add_tile(2, 0, "pair2")
        for q in range(QUARTERS):
            block_sums("r", q, (3, 0) if q % 2 else (1, 2))
        quantize_block("i", 0, pair_buffers(("pair0", "pair1")))
        quantize_block("i", 1, pair_buffers(("after_block0", "after_block1")))

        after = keep.tile([P, 2, PACK, P], F32, name="after_block1", align_bytes=256)
        strip_power[2, 1] = after[:, 0]
        strip_power[3, 0] = after[:, 1]
        add_strip(2, 1, slice(0, P), strip_power[2, 1])
        h_scales[0] = keep.tile([P, S], U8, name="after_block0", align_bytes=256)
        quantize_envelope(0, 0, 2 * QUARTER)
        add_strip(3, 0, slice(0, P), strip_power[3, 0])
        halves = (slice(0, P), slice(P, QUARTER))
        block_sums("i", 0, (1, 2))
        for u in range(2):
            add_block(0, slice(u, u + 1))
        block_sums("i", 1, (3, 0))
        for u in range(2):
            add_block(1, slice(u, u + 1))
        root_block(0)
        quantize_envelope(1, 0, QUARTER)
        add_tile(3, 1, "block_squares_i1")
        block_sums("i", 2, (1, 2), "block_squares_r0")
        for u in range(2):
            add_block(2, slice(u, u + 1))
        first = [cell_sums(0, QUARTER, c0, 2, (0, 1), 6 + c0 // 2) for c0 in (0, 2)]
        root_block(1)
        scale_and_store(first[0], "pair0")
        quantize_envelope(1, QUARTER, QUARTER)
        scale_and_store(first[1], "pair1")
        hold_envelope(0, 2 * QUARTER, QUARTER, "block_squares_r1")
        for i in range(2):
            turn_and_root(2, i, 4 + i)
        quantize_envelope(0, 2 * QUARTER, QUARTER)
        second = [cell_sums(QUARTER, QUARTER, c0, 2, (0, 1), (3, 0)[c0 // 2]) for c0 in (0, 2)]
        scale_and_store(second[0], "pair3")
        root_block(2)
        scale_and_store(second[1], "third_rounded0")
        quantize_envelope(1, 2 * QUARTER, QUARTER)
        block_sums("i", 3, (1, 2), "block_squares_r2")
        for u in range(2):
            add_block(3, slice(u, u + 1))
        third = [cell_sums(2 * QUARTER, QUARTER, c0, 2, (0, 1), 6 + c0 // 2) for c0 in (0, 2)]
        for i in range(2):
            hold_envelope(0, 3 * QUARTER + i * P, P, "rounded0_unit%d" % i)
            turn_and_root(3, i, 4 + i)
            quantize_envelope(0, 3 * QUARTER + i * P, P)
            unread = in_bank(4 + i, [P, PASS])
            cols = slice(3 * QUARTER + (i + 1) * P - PASS, 3 * QUARTER + (i + 1) * P)
            nc.tensor.matmul_mx(
                out=unread[:],
                lhsT=w3_codes[:, 0, 0:P].bitcast(E4M3),
                lhsT_scale=w3_planes[:, 0:P],
                rhs=h_codes[0][:, cols].bitcast(E4M3),
                rhs_scale=h_scales[0][:, cols],
                start=True,
                stop=True,
            )
            scale_and_store(third[i], "rounded0_unit%d" % i)
        for i in range(2):
            j0 = 3 * QUARTER + i * P
            root_block(3, halves[i])
            quantize_envelope(1, j0, P)
        for i in range(2):
            j0 = 3 * QUARTER + i * P
            scale_and_store(cell_sums(j0, P, 0, 2, (0, 1), (3, 1)[i]), ("first_strip0", "second_rounded1")[i])
            scale_and_store(cell_sums(j0, P, 2, 2, (0, 1), (0, 2)[i]), ("first_rounded0", "second_rounded0")[i], True)
